import numpy as np
import ml_dtypes


def mxq(x, axis, fmt="e4m3"):
    dtype, down = {"e4m3": (ml_dtypes.float8_e4m3fn, 7), "e5m2": (ml_dtypes.float8_e5m2, 14)}[fmt]
    v = np.moveaxis(np.asarray(x, np.float32).astype(ml_dtypes.bfloat16).astype(np.float64), axis, -1)
    blocks = v.reshape(v.shape[:-1] + (-1, 32))
    amax = np.abs(blocks).max(-1, keepdims=True)
    byte = np.maximum(np.where(amax > 0, np.frexp(amax)[1] - 1 + 127, 0) - down, 1)
    scale = np.exp2(byte - 127.0)
    codes = (blocks / scale).astype(np.float32).astype(dtype).astype(np.float64)
    return np.moveaxis((codes * scale).reshape(v.shape), -1, axis)


WIDE = False


def mx_kscale(k):
    if not WIDE:
        return np.ones(k)
    levels = np.array([10, -10, 5, -5, 0])
    if k % 512:
        return np.exp2(np.random.permutation(np.resize(levels, k // 32))).repeat(32)
    a = np.empty((k // 512, 16))
    for p in range(k // 512):
        a[p, :8] = np.random.permutation(np.resize(levels, 8))
        for g in range(8):
            far = levels[np.abs(levels - a[p, g]) >= 10]
            a[p, g + 8] = far[np.random.randint(len(far))]
    return np.exp2(a.ravel()).repeat(32)


def f64(x):
    return np.asarray(x).astype(np.float64)


def striped(idx):
    return np.tile(idx.reshape(-1, 16).T, (8, 1)).astype(np.uint16)


def unstriped(offs):
    return offs[:16].T.reshape(-1).astype(np.int64)


def pack_weight(w):
    k, n = w.shape
    w = f64(np.asarray(w, np.float32).astype(ml_dtypes.bfloat16)).reshape(k // 32, 32, n)
    amax = np.abs(w).max(1)
    byte = np.clip(np.where(amax > 0, np.frexp(amax)[1] - 1 + 127 - 7, 1), 1, 254)
    scaled = (w * np.exp2(127.0 - byte)[:, None, :]).reshape(k, n).astype(np.float32)
    words = np.ascontiguousarray(scaled.reshape(k // 512, 128, 4, n).transpose(0, 1, 3, 2)).astype(ml_dtypes.float8_e4m3fn).view(np.uint8)
    return words, np.ascontiguousarray(byte.astype(np.uint8).reshape(k // 512, 16, n))


def unpack_weight(words, scales):
    g, p, n, _ = words.shape
    vals = np.ascontiguousarray(words).view(ml_dtypes.float8_e4m3fn).astype(np.float64) * np.repeat(np.exp2(scales.astype(np.float64) - 127.0), 8, axis=1)[..., None]
    return vals.transpose(0, 1, 3, 2).reshape(g * 512, n)


def sigmoid(v):
    return 1.0 / (1.0 + np.exp(-np.maximum(v, -700.0)))


K, T, S, W, N = 512, 1024, 512, 1024, 128


def setup_inputs():
    n = np.random.standard_normal
    s = mx_kscale(K)[:, None]
    packed_xT = pack_weight(n((K, T)) * s)
    packed_eT = pack_weight(n((K, W)) * s)
    return {
        "x_words": packed_xT[0],
        "x_scales": packed_xT[1],
        "e_words": packed_eT[0],
        "e_scales": packed_eT[1],
        "wfo": (n((K, N)) / np.sqrt(2 * K) / s).astype(np.float32),
        "vfo": (n((K, N)) / np.sqrt(2 * K) / s).astype(np.float32),
        "wex": (n((K, N)) / np.sqrt(2 * K) / s).astype(np.float32),
        "vex": (n((K, N)) / np.sqrt(2 * K) / s).astype(np.float32),
        "wca": (n((K, N)) / np.sqrt(2 * K) / s).astype(np.float32),
        "vca": (n((K, N)) / np.sqrt(2 * K) / s).astype(np.float32),
        "cell": (n((N, T))).astype(np.float32),
        "offs": striped(np.random.permutation(T)[:S]),
        "tok": striped(np.random.permutation(W)[:S]),
    }


def reference(x_words, x_scales, e_words, e_scales, wfo, vfo, wex, vex, wca, vca, cell, offs, tok):
    xq = unpack_weight(x_words, x_scales)[:, unstriped(offs)]
    e_tok = unpack_weight(e_words, e_scales)[:, unstriped(tok)]
    b = sigmoid(mxq(f64(wex), 0, "e4m3").T @ xq + mxq(f64(vex), 0, "e4m3").T @ e_tok)
    old = f64(cell)[:, unstriped(offs)]
    f = sigmoid(mxq(f64(wfo), 0, "e4m3").T @ xq + mxq(f64(vfo), 0, "e4m3").T @ e_tok)
    g = np.tanh(mxq(f64(wca), 0, "e4m3").T @ xq + mxq(f64(vca), 0, "e4m3").T @ e_tok)
    new = old * f + g - (g * f)
    return b * np.tanh(new)

@@ -1,0 +1,163 @@
+from contextlib import ExitStack
+
+import concourse.mybir as mybir
+
+F32 = mybir.dt.float32
+BF16 = mybir.dt.bfloat16
+I32 = mybir.dt.int32
+U32 = mybir.dt.uint32
+U16 = mybir.dt.uint16
+U8 = mybir.dt.uint8
+FP8X4 = mybir.dt.float8_e4m3fn_x4
+ACT = mybir.ActivationFunctionType
+ALU = mybir.AluOpType
+
+P = 128
+PACK = 4
+TABLE = 1024
+PICKS = 512
+UNITS = 128
+HALF = 256
+FLOPS = 2 * 6 * 512 * UNITS * PICKS
+
+
+def tile_picked_zlstm_cifg_p_kernel(
+    tc, x_words, x_scales, e_words, e_scales, wfo, vfo, wex, vex, wca, vca, cell, offs, tok, out
+):
+    nc = tc.nc
+    with ExitStack() as ctx:
+        keep = ctx.enter_context(tc.tile_pool(name="keep", bufs=1))
+        psum = ctx.enter_context(tc.psum_pool(name="psum", bufs=1))
+
+        def sb(name, shape, dtype):
+            return keep.tile(shape, dtype, name=name, align_bytes=64)
+
+        offs_sb = keep.tile([P, PICKS // 16], U16, name="offs_sb")
+        tok_sb = keep.tile([P, PICKS // 16], U16, name="tok_sb")
+        xs_tab = sb("xs_tab", [P, TABLE], U8)
+        es_tab = sb("es_tab", [P, TABLE], U8)
+        xw_tab = sb("xw_tab", [P, TABLE], I32)
+        ew_tab = sb("ew_tab", [P, TABLE], I32)
+        cell_sb = sb("cell_sb", [P, TABLE], F32)
+
+        def load_scales(queue, table, scales, quadrants):
+            for q in quadrants:
+                queue.dma_start(
+                    out=table[32 * q : 32 * q + 4, :].bitcast(I32),
+                    in_=scales[0, 4 * q : 4 * q + 4, :].bitcast(I32),
+                )
+
+        def load_words(table, words):
+            nc.sync.dma_start(out=table[:], in_=words[0].rearrange("p n t -> p (n t)").bitcast(I32))
+
+        raw = {}
+
+        def load_weight(name, w):
+            raw[name] = sb("raw_" + name, [P, PACK, UNITS], F32)
+            nc.sync.dma_start(out=raw[name][:], in_=w.rearrange("(p j) m -> p j m", j=PACK))
+
+        nc.vector.memset(xs_tab[:].bitcast(I32), 0)
+        nc.vector.memset(es_tab[:].bitcast(I32), 0)
+        warm_in = sb("warm_in", [P, 1], F32)
+        warm_out = sb("warm_out", [P, 1], F32)
+        nc.gpsimd.memset(warm_in[:], 0.0)
+        nc.scalar.activation(warm_out[:], warm_in[:], ACT.Sigmoid)
+        nc.sync.dma_start(offs_sb[:], offs)
+        load_scales(nc.sync, xs_tab, x_scales, range(4))
+        load_words(xw_tab, x_words)
+        load_weight("wca", wca)
+        load_weight("vca", vca)
+        nc.sync.dma_start(tok_sb[:], tok)
+        load_scales(nc.sync, es_tab, e_scales, range(3))
+        load_words(ew_tab, e_words)
+        load_weight("wfo", wfo)
+        load_weight("vfo", vfo)
+        load_scales(nc.sync, es_tab, e_scales, range(3, 4))
+        load_weight("wex", wex)
+        load_weight("vex", vex)
+        nc.sync.dma_start(out=cell_sb[:], in_=cell)
+
+        codes, scales = {}, {}
+
+        def quantise(names):
+            tag = "_".join(names)
+            n = len(names)
+            grouped = sb("grouped_" + tag, [P, n, UNITS * PACK], BF16)
+            for i, name in enumerate(names):
+                nc.scalar.copy(
+                    out=grouped[:, i, :].rearrange("p (c i t) -> p c t i", i=4, t=PACK),
+                    in_=raw[name][:].rearrange("p t (c i) -> p c t i", i=4),
+                )
+            cw = sb("codes_" + tag, [P, n * UNITS], U32)
+            cs = sb("scales_" + tag, [P, n * UNITS], U8)
+            nc.vector.quantize_mx(out=cw[:].bitcast(FP8X4), scales=cs[:], in_=grouped[:].rearrange("p n w -> p (n w)"))
+            for i, name in enumerate(names):
+                codes[name] = cw[:, i * UNITS : (i + 1) * UNITS]
+                scales[name] = cs[:, i * UNITS : (i + 1) * UNITS]
+
+        def part(lst, h):
+            return lst[:, h * HALF // 16 : (h + 1) * HALF // 16]
+
+        xs = sb("xs", [P, PICKS], U8)
+        xw = sb("xw", [P, PICKS], U32)
+        nc.vector.tensor_copy(xs[:], xs_tab[:].indirect(offs_sb[:]))
+        nc.vector.tensor_copy(xw[:], xw_tab[:].bitcast(U32).indirect(offs_sb[:]))
+        quantise(["wca", "vca"])
+
+        acc = {}
+
+        def product(gate, name, h, words, bytes_, first):
+            if first:
+                acc[gate, h] = psum.tile([P, HALF], F32, name=f"acc_{gate}{h}")
+            nc.tensor.matmul_mx(
+                out=acc[gate, h][:],
+                lhsT=codes[name].bitcast(FP8X4),
+                lhsT_scale=scales[name],
+                rhs=words.bitcast(FP8X4),
+                rhs_scale=bytes_,
+                start=first,
+                stop=not first,
+            )
+
+        def cols(h):
+            return slice(h * HALF, (h + 1) * HALF)
+
+        for h in range(2):
+            product("g", "wca", h, xw[:, cols(h)], xs[:, cols(h)], True)
+
+        ew = sb("ew", [P, PICKS], U32)
+        nc.vector.tensor_copy(ew[:], ew_tab[:].bitcast(U32).indirect(tok_sb[:]))
+        quantise(["wfo", "vfo"])
+        for h in range(2):
+            product("f", "wfo", h, xw[:, cols(h)], xs[:, cols(h)], True)
+        es, g, f, b, fresh, kept, new, th = {}, {}, {}, {}, {}, {}, {}, {}
+        for h in range(2):
+            es[h] = sb(f"es{h}", [P, HALF], U8)
+            nc.vector.tensor_copy(es[h][:], es_tab[:].indirect(part(tok_sb, h)))
+            product("g", "vca", h, ew[:, cols(h)], es[h][:], False)
+            product("f", "vfo", h, ew[:, cols(h)], es[h][:], False)
+            g[h] = sb(f"g{h}", [P, HALF], F32)
+            nc.scalar.activation(g[h][:], acc["g", h][:], ACT.Tanh)
+            f[h] = sb(f"f{h}", [P, HALF], F32)
+            nc.scalar.activation(f[h][:], acc["f", h][:], ACT.Sigmoid)
+        quantise(["wex", "vex"])
+        for h in range(2):
+            product("b", "wex", h, xw[:, cols(h)], xs[:, cols(h)], True)
+            product("b", "vex", h, ew[:, cols(h)], es[h][:], False)
+            b[h] = sb(f"b{h}", [P, HALF], F32)
+            nc.scalar.activation(b[h][:], acc["b", h][:], ACT.Sigmoid)
+        for h in range(2):
+            fresh[h] = sb(f"fresh{h}", [P, HALF], F32)
+            nc.vector.scalar_tensor_tensor(fresh[h][:], f[h][:], 1.0, g[h][:], ALU.subtract, ALU.mult)
+        for h in range(2):
+            kept[h] = sb(f"kept{h}", [P, HALF], F32)
+            nc.vector.tensor_tensor(kept[h][:], cell_sb[:].indirect(part(offs_sb, h)), f[h][:], ALU.mult)
+        for h in range(2):
+            new[h] = sb(f"new{h}", [P, HALF], F32)
+            nc.vector.tensor_tensor(new[h][:], kept[h][:], fresh[h][:], ALU.subtract)
+            th[h] = sb(f"th{h}", [P, HALF], F32)
+            nc.scalar.activation(th[h][:], new[h][:], ACT.Tanh)
+        for h in range(2):
+            res = sb(f"res{h}", [P, HALF], F32)
+            nc.vector.tensor_tensor(res[:], b[h][:], th[h][:], ALU.mult)
+            nc.sync.dma_start(out=out[:, cols(h)], in_=res[:])

@@ -29,8 +29,8 @@ def tile_picked_zlstm_cifg_p_kernel(
         keep = ctx.enter_context(tc.tile_pool(name="keep", bufs=1))
         psum = ctx.enter_context(tc.psum_pool(name="psum", bufs=1))
 
-        def sb(name, shape, dtype):
-            return keep.tile(shape, dtype, name=name, align_bytes=64)
+        def sb(name, shape, dtype, tag=None):
+            return keep.tile(shape, dtype, name=name, tag=tag or name, align_bytes=64)
 
         offs_sb = keep.tile([P, PICKS // 16], U16, name="offs_sb")
         tok_sb = keep.tile([P, PICKS // 16], U16, name="tok_sb")
@@ -60,29 +60,31 @@ def tile_picked_zlstm_cifg_p_kernel(
         nc.vector.memset(es_tab[:].bitcast(I32), 0)
         warm_in = sb("warm_in", [P, 1], F32)
         warm_out = sb("warm_out", [P, 1], F32)
-        nc.gpsimd.memset(warm_in[:], 0.0)
-        nc.scalar.activation(warm_out[:], warm_in[:], ACT.Sigmoid)
+        nc.vector.memset(warm_in[:], 0.0)
         nc.sync.dma_start(offs_sb[:], offs)
-        load_scales(nc.sync, xs_tab, x_scales, range(4))
+        load_scales(nc.sync, xs_tab, x_scales, range(2))
+        load_scales(nc.scalar, xs_tab, x_scales, range(2, 4))
+        nc.scalar.activation(warm_out[:], warm_in[:], ACT.Sigmoid)
         load_words(xw_tab, x_words)
         load_weight("wca", wca)
-        load_weight("vca", vca)
+        load_weight("wfo", wfo)
         nc.sync.dma_start(tok_sb[:], tok)
         load_scales(nc.sync, es_tab, e_scales, range(3))
         load_words(ew_tab, e_words)
-        load_weight("wfo", wfo)
+        load_weight("vca", vca)
         load_weight("vfo", vfo)
         load_scales(nc.sync, es_tab, e_scales, range(3, 4))
         load_weight("wex", wex)
         load_weight("vex", vex)
         nc.sync.dma_start(out=cell_sb[:], in_=cell)
 
-        codes, scales = {}, {}
+        codes, scales, staged = {}, {}, {}
 
         def quantise(names):
             tag = "_".join(names)
             n = len(names)
             grouped = sb("grouped_" + tag, [P, n, UNITS * PACK], BF16)
+            staged[tag] = grouped
             for i, name in enumerate(names):
                 nc.scalar.copy(
                     out=grouped[:, i, :].rearrange("p (c i t) -> p c t i", i=4, t=PACK),
@@ -102,7 +104,7 @@ def tile_picked_zlstm_cifg_p_kernel(
         xw = sb("xw", [P, PICKS], U32)
         nc.vector.tensor_copy(xs[:], xs_tab[:].indirect(offs_sb[:]))
         nc.vector.tensor_copy(xw[:], xw_tab[:].bitcast(U32).indirect(offs_sb[:]))
-        quantise(["wca", "vca"])
+        quantise(["wca", "wfo"])
 
         acc = {}
 
@@ -124,37 +126,37 @@ def tile_picked_zlstm_cifg_p_kernel(
 
         for h in range(2):
             product("g", "wca", h, xw[:, cols(h)], xs[:, cols(h)], True)
+            product("f", "wfo", h, xw[:, cols(h)], xs[:, cols(h)], True)
 
         ew = sb("ew", [P, PICKS], U32)
         nc.vector.tensor_copy(ew[:], ew_tab[:].bitcast(U32).indirect(tok_sb[:]))
-        quantise(["wfo", "vfo"])
-        for h in range(2):
-            product("f", "wfo", h, xw[:, cols(h)], xs[:, cols(h)], True)
         es, g, f, b, fresh, kept, new, th = {}, {}, {}, {}, {}, {}, {}, {}
         for h in range(2):
-            es[h] = sb(f"es{h}", [P, HALF], U8)
+            es[h] = sb(f"es{h}", [P, HALF], U8, "es0" if h == 0 else "grouped_vca_vfo")
             nc.vector.tensor_copy(es[h][:], es_tab[:].indirect(part(tok_sb, h)))
+            if h == 0:
+                quantise(["vca", "vfo"])
             product("g", "vca", h, ew[:, cols(h)], es[h][:], False)
             product("f", "vfo", h, ew[:, cols(h)], es[h][:], False)
-            g[h] = sb(f"g{h}", [P, HALF], F32)
-            nc.scalar.activation(g[h][:], acc["g", h][:], ACT.Tanh)
-            f[h] = sb(f"f{h}", [P, HALF], F32)
-            nc.scalar.activation(f[h][:], acc["f", h][:], ACT.Sigmoid)
         quantise(["wex", "vex"])
+        for h in range(2):
+            g[h] = raw["wex"][:].rearrange("p j m -> p (j m)")[:, cols(h)]
+            nc.scalar.activation(g[h], acc["g", h][:], ACT.Tanh)
+            f[h] = raw["vex"][:].rearrange("p j m -> p (j m)")[:, cols(h)]
+            nc.scalar.activation(f[h], acc["f", h][:], ACT.Sigmoid)
         for h in range(2):
             product("b", "wex", h, xw[:, cols(h)], xs[:, cols(h)], True)
             product("b", "vex", h, ew[:, cols(h)], es[h][:], False)
             b[h] = sb(f"b{h}", [P, HALF], F32)
             nc.scalar.activation(b[h][:], acc["b", h][:], ACT.Sigmoid)
         for h in range(2):
-            fresh[h] = sb(f"fresh{h}", [P, HALF], F32)
-            nc.vector.scalar_tensor_tensor(fresh[h][:], f[h][:], 1.0, g[h][:], ALU.subtract, ALU.mult)
-        for h in range(2):
+            fresh[h] = staged["wex_vex"][:].rearrange("p n w -> p (n w)").bitcast(F32)[:, cols(h)]
+            nc.vector.scalar_tensor_tensor(fresh[h], f[h], 1.0, g[h], ALU.subtract, ALU.mult)
             kept[h] = sb(f"kept{h}", [P, HALF], F32)
-            nc.vector.tensor_tensor(kept[h][:], cell_sb[:].indirect(part(offs_sb, h)), f[h][:], ALU.mult)
+            nc.vector.tensor_tensor(kept[h][:], cell_sb[:].indirect(part(offs_sb, h)), f[h], ALU.mult)
         for h in range(2):
             new[h] = sb(f"new{h}", [P, HALF], F32)
-            nc.vector.tensor_tensor(new[h][:], kept[h][:], fresh[h][:], ALU.subtract)
+            nc.vector.tensor_tensor(new[h][:], kept[h][:], fresh[h], ALU.subtract)
             th[h] = sb(f"th{h}", [P, HALF], F32)
             nc.scalar.activation(th[h][:], new[h][:], ACT.Tanh)
         for h in range(2):

@@ -29,7 +29,12 @@ def tile_picked_zlstm_cifg_p_kernel(
         keep = ctx.enter_context(tc.tile_pool(name="keep", bufs=1))
         psum = ctx.enter_context(tc.psum_pool(name="psum", bufs=1))
 
+        reuse = ctx.enter_context(tc.tile_pool(name="reuse", bufs=1))
+        places = {"raw_vfo": 0, "ew1": 0, "old": 1024, "grouped_bx": 4096, "grouped_be": 4096}
+
         def sb(name, shape, dtype, tag=None):
+            if name in places:
+                return reuse.tile(shape, dtype, name=name, align_bytes=64, offset=places[name])
             return keep.tile(shape, dtype, name=name, tag=tag or name, align_bytes=64)
 
         offs_sb = keep.tile([P, PICKS // 16], U16, name="offs_sb")
@@ -51,60 +56,38 @@ def tile_picked_zlstm_cifg_p_kernel(
             nc.sync.dma_start(out=table[:], in_=words[0].rearrange("p n t -> p (n t)").bitcast(I32))
 
         raw = {}
+        shared = sb("shared", [P, 3 * HALF], F32)
 
         def load_weight(name, w):
-            raw[name] = sb("raw_" + name, [P, PACK, UNITS], F32)
-            nc.sync.dma_start(out=raw[name][:], in_=w.rearrange("(p j) m -> p j m", j=PACK))
-
-        nc.vector.memset(xs_tab[:].bitcast(I32), 0)
-        nc.vector.memset(es_tab[:].bitcast(I32), 0)
-        warm_in = sb("warm_in", [P, 1], F32)
-        warm_out = sb("warm_out", [P, 1], F32)
-        nc.vector.memset(warm_in[:], 0.0)
-        nc.sync.dma_start(offs_sb[:], offs)
-        load_scales(nc.sync, xs_tab, x_scales, range(2))
-        load_scales(nc.scalar, xs_tab, x_scales, range(2, 4))
-        nc.scalar.activation(warm_out[:], warm_in[:], ACT.Sigmoid)
-        load_words(xw_tab, x_words)
-        load_weight("wca", wca)
-        load_weight("wfo", wfo)
-        nc.sync.dma_start(tok_sb[:], tok)
-        load_scales(nc.sync, es_tab, e_scales, range(3))
-        load_words(ew_tab, e_words)
-        load_weight("vca", vca)
-        load_weight("vfo", vfo)
-        load_scales(nc.sync, es_tab, e_scales, range(3, 4))
-        load_weight("wex", wex)
-        load_weight("vex", vex)
-        nc.sync.dma_start(out=cell_sb[:], in_=cell)
+            if name == "vex":
+                raw[name] = shared[:, HALF:]
+            else:
+                raw[name] = sb("raw_" + name, [P, PACK * UNITS], F32)[:]
+            nc.sync.dma_start(out=raw[name], in_=w.rearrange("(p j) m -> p (j m)", j=PACK))
 
         codes, scales, staged = {}, {}, {}
 
-        def quantise(names):
-            tag = "_".join(names)
+        def cast(group, names, name, engine):
+            if group not in staged:
+                staged[group] = sb("grouped_" + group, [P, len(names) * UNITS * PACK], BF16)
+            i = names.index(name)
+            dst = staged[group][:, i * UNITS * PACK : (i + 1) * UNITS * PACK].rearrange("p (c i t) -> p c t i", i=4, t=PACK)
+            src = raw[name].rearrange("p (t c i) -> p c t i", t=PACK, i=4)
+            if engine == "scalar":
+                nc.scalar.copy(out=dst, in_=src)
+            elif engine == "vector":
+                nc.vector.tensor_copy(out=dst, in_=src)
+            else:
+                nc.gpsimd.tensor_copy(out=dst, in_=src)
+
+        def quantise(group, names):
             n = len(names)
-            grouped = sb("grouped_" + tag, [P, n, UNITS * PACK], BF16)
-            staged[tag] = grouped
-            for i, name in enumerate(names):
-                nc.scalar.copy(
-                    out=grouped[:, i, :].rearrange("p (c i t) -> p c t i", i=4, t=PACK),
-                    in_=raw[name][:].rearrange("p t (c i) -> p c t i", i=4),
-                )
-            cw = sb("codes_" + tag, [P, n * UNITS], U32)
-            cs = sb("scales_" + tag, [P, n * UNITS], U8)
-            nc.vector.quantize_mx(out=cw[:].bitcast(FP8X4), scales=cs[:], in_=grouped[:].rearrange("p n w -> p (n w)"))
+            cw = sb("codes_" + group, [P, n * UNITS], U32)
+            cs = sb("scales_" + group, [P, n * UNITS], U8)
+            nc.vector.quantize_mx(out=cw[:].bitcast(FP8X4), scales=cs[:], in_=staged[group][:])
             for i, name in enumerate(names):
                 codes[name] = cw[:, i * UNITS : (i + 1) * UNITS]
                 scales[name] = cs[:, i * UNITS : (i + 1) * UNITS]
-
-        def part(lst, h):
-            return lst[:, h * HALF // 16 : (h + 1) * HALF // 16]
-
-        xs = sb("xs", [P, PICKS], U8)
-        xw = sb("xw", [P, PICKS], U32)
-        nc.vector.tensor_copy(xs[:], xs_tab[:].indirect(offs_sb[:]))
-        nc.vector.tensor_copy(xw[:], xw_tab[:].bitcast(U32).indirect(offs_sb[:]))
-        quantise(["wca", "wfo"])
 
         acc = {}
 
@@ -124,42 +107,89 @@ def tile_picked_zlstm_cifg_p_kernel(
         def cols(h):
             return slice(h * HALF, (h + 1) * HALF)
 
+        def clock(name, ap):
+            c = sb("clock_" + name, [P, 1], ap.dtype)
+            nc.gpsimd.tensor_copy(c[:], ap)
+
+        nc.vector.memset(xs_tab[:].bitcast(I32), 0)
+        nc.gpsimd.memset(es_tab[:].bitcast(I32), 0)
+        warm_in = sb("warm_in", [P, 1], F32)
+        warm_out = sb("warm_out", [P, 1], F32)
+        nc.vector.memset(warm_in[:], 0.0)
+        nc.scalar.activation(warm_out[:], warm_in[:], ACT.Sigmoid)
+        nc.sync.dma_start(offs_sb[:], offs)
+        load_words(xw_tab, x_words)
+        load_scales(nc.sync, xs_tab, x_scales, range(4))
+        load_scales(nc.gpsimd, es_tab, e_scales, range(1))
+        load_weight("wca", wca)
+        load_weight("wfo", wfo)
+        load_words(ew_tab, e_words)
+        nc.sync.dma_start(tok_sb[:], tok)
+        load_scales(nc.sync, es_tab, e_scales, range(1, 4))
+        load_weight("vca", vca)
+        load_weight("vfo", vfo)
+        load_weight("wex", wex)
+        nc.sync.dma_start(out=cell_sb[:], in_=cell)
+        load_weight("vex", vex)
+
+        xs = sb("xs", [P, PICKS], U8)
+        xw = sb("xw", [P, PICKS], U32)
+        es = sb("es", [P, PICKS], U8)
+        ew = {}
+
+        def prepare(group, names):
+            for name in names:
+                cast(group, names, name, "scalar")
+            quantise(group, names)
+
+        def gather_ew(h):
+            ew[h] = sb(f"ew{h}", [P, HALF], U32)
+            nc.vector.tensor_copy(ew[h][:], ew_tab[:].bitcast(U32).indirect(tok_sb[:, h * HALF // 16 : (h + 1) * HALF // 16]))
+
+        nc.vector.tensor_copy(xw[:], xw_tab[:].bitcast(U32).indirect(offs_sb[:]))
+        nc.vector.tensor_copy(xs[:], xs_tab[:].indirect(offs_sb[:]))
+        prepare("x", ["wca", "wfo"])
         for h in range(2):
             product("g", "wca", h, xw[:, cols(h)], xs[:, cols(h)], True)
             product("f", "wfo", h, xw[:, cols(h)], xs[:, cols(h)], True)
-
-        ew = sb("ew", [P, PICKS], U32)
-        nc.vector.tensor_copy(ew[:], ew_tab[:].bitcast(U32).indirect(tok_sb[:]))
-        es, g, f, b, fresh, kept, new, th = {}, {}, {}, {}, {}, {}, {}, {}
+        gather_ew(0)
+        nc.vector.tensor_copy(es[:], es_tab[:].indirect(tok_sb[:]))
+        prepare("e", ["vca", "vfo"])
+        gather_ew(1)
         for h in range(2):
-            es[h] = sb(f"es{h}", [P, HALF], U8, "es0" if h == 0 else "grouped_vca_vfo")
-            nc.vector.tensor_copy(es[h][:], es_tab[:].indirect(part(tok_sb, h)))
-            if h == 0:
-                quantise(["vca", "vfo"])
-            product("g", "vca", h, ew[:, cols(h)], es[h][:], False)
-            product("f", "vfo", h, ew[:, cols(h)], es[h][:], False)
-        quantise(["wex", "vex"])
-        for h in range(2):
-            g[h] = raw["wex"][:].rearrange("p j m -> p (j m)")[:, cols(h)]
-            nc.scalar.activation(g[h], acc["g", h][:], ACT.Tanh)
-            f[h] = raw["vex"][:].rearrange("p j m -> p (j m)")[:, cols(h)]
-            nc.scalar.activation(f[h], acc["f", h][:], ACT.Sigmoid)
+            product("g", "vca", h, ew[h][:], es[:, cols(h)], False)
+            product("f", "vfo", h, ew[h][:], es[:, cols(h)], False)
+        prepare("bx", ["wex"])
         for h in range(2):
             product("b", "wex", h, xw[:, cols(h)], xs[:, cols(h)], True)
-            product("b", "vex", h, ew[:, cols(h)], es[h][:], False)
-            b[h] = sb(f"b{h}", [P, HALF], F32)
-            nc.scalar.activation(b[h][:], acc["b", h][:], ACT.Sigmoid)
+        old = sb("old", [P, PICKS], F32)
+        nc.vector.tensor_copy(old[:], cell_sb[:].indirect(offs_sb[:]))
+        g = [sb("g0", [P, HALF], F32)[:], shared[:, cols(2)]]
+        f = shared[:, :PICKS]
+        fresh = sb("fresh", [P, PICKS], F32)
+        kept = sb("kept", [P, PICKS], F32)
+        new = sb("new", [P, PICKS], F32)
+        th = sb("th", [P, PICKS], F32)
+        b = sb("b", [P, PICKS], F32)
+
+        def gates(h):
+            nc.scalar.activation(g[h], acc["g", h][:], ACT.Tanh)
+            nc.scalar.activation(f[:, cols(h)], acc["f", h][:], ACT.Sigmoid)
+
+        gates(0)
+        cast("be", ["vex"], "vex", "scalar")
+        gates(1)
+        nc.vector.scalar_tensor_tensor(fresh[:, cols(0)], f[:, cols(0)], 1.0, g[0], ALU.subtract, ALU.mult)
+        quantise("be", ["vex"])
         for h in range(2):
-            fresh[h] = staged["wex_vex"][:].rearrange("p n w -> p (n w)").bitcast(F32)[:, cols(h)]
-            nc.vector.scalar_tensor_tensor(fresh[h], f[h], 1.0, g[h], ALU.subtract, ALU.mult)
-            kept[h] = sb(f"kept{h}", [P, HALF], F32)
-            nc.vector.tensor_tensor(kept[h][:], cell_sb[:].indirect(part(offs_sb, h)), f[h], ALU.mult)
+            product("b", "vex", h, ew[h][:], es[:, cols(h)], False)
+            nc.scalar.activation(b[:, cols(h)], acc["b", h][:], ACT.Sigmoid)
+        nc.vector.tensor_tensor(kept[:], old[:], f, ALU.mult)
+        nc.vector.scalar_tensor_tensor(fresh[:, cols(1)], f[:, cols(1)], 1.0, g[1], ALU.subtract, ALU.mult)
         for h in range(2):
-            new[h] = sb(f"new{h}", [P, HALF], F32)
-            nc.vector.tensor_tensor(new[h][:], kept[h][:], fresh[h], ALU.subtract)
-            th[h] = sb(f"th{h}", [P, HALF], F32)
-            nc.scalar.activation(th[h][:], new[h][:], ACT.Tanh)
+            nc.vector.tensor_tensor(new[:, cols(h)], kept[:, cols(h)], fresh[:, cols(h)], ALU.subtract)
+            nc.scalar.activation(th[:, cols(h)], new[:, cols(h)], ACT.Tanh)
         for h in range(2):
             res = sb(f"res{h}", [P, HALF], F32)
-            nc.vector.tensor_tensor(res[:], b[h][:], th[h][:], ALU.mult)
+            nc.vector.tensor_tensor(res[:], b[:, cols(h)], th[:, cols(h)], ALU.mult)
             nc.sync.dma_start(out=out[:, cols(h)], in_=res[:])

@@ -30,7 +30,7 @@ def tile_picked_zlstm_cifg_p_kernel(
         psum = ctx.enter_context(tc.psum_pool(name="psum", bufs=1))
 
         reuse = ctx.enter_context(tc.tile_pool(name="reuse", bufs=1))
-        places = {"raw_vfo": 0, "ew1": 0, "old": 1024, "grouped_bx": 4096, "grouped_be": 4096}
+        places = {"raw_vfo": 0, "ew1": 0}
 
         def sb(name, shape, dtype, tag=None):
             if name in places:
@@ -56,14 +56,10 @@ def tile_picked_zlstm_cifg_p_kernel(
             nc.sync.dma_start(out=table[:], in_=words[0].rearrange("p n t -> p (n t)").bitcast(I32))
 
         raw = {}
-        shared = sb("shared", [P, 3 * HALF], F32)
 
         def load_weight(name, w):
-            if name == "vex":
-                raw[name] = shared[:, HALF:]
-            else:
-                raw[name] = sb("raw_" + name, [P, PACK * UNITS], F32)[:]
-            nc.sync.dma_start(out=raw[name], in_=w.rearrange("(p j) m -> p (j m)", j=PACK))
+            raw[name] = sb("raw_" + name, [P, PACK * UNITS], F32)
+            nc.sync.dma_start(out=raw[name][:], in_=w.rearrange("(p j) m -> p (j m)", j=PACK))
 
         codes, scales, staged = {}, {}, {}
 
@@ -72,7 +68,7 @@ def tile_picked_zlstm_cifg_p_kernel(
                 staged[group] = sb("grouped_" + group, [P, len(names) * UNITS * PACK], BF16)
             i = names.index(name)
             dst = staged[group][:, i * UNITS * PACK : (i + 1) * UNITS * PACK].rearrange("p (c i t) -> p c t i", i=4, t=PACK)
-            src = raw[name].rearrange("p (t c i) -> p c t i", t=PACK, i=4)
+            src = raw[name][:].rearrange("p (t c i) -> p c t i", t=PACK, i=4)
             if engine == "scalar":
                 nc.scalar.copy(out=dst, in_=src)
             elif engine == "vector":
@@ -129,8 +125,8 @@ def tile_picked_zlstm_cifg_p_kernel(
         load_weight("vca", vca)
         load_weight("vfo", vfo)
         load_weight("wex", wex)
-        nc.sync.dma_start(out=cell_sb[:], in_=cell)
         load_weight("vex", vex)
+        nc.sync.dma_start(out=cell_sb[:], in_=cell)
 
         xs = sb("xs", [P, PICKS], U8)
         xw = sb("xw", [P, PICKS], U32)
@@ -159,33 +155,24 @@ def tile_picked_zlstm_cifg_p_kernel(
         for h in range(2):
             product("g", "vca", h, ew[h][:], es[:, cols(h)], False)
             product("f", "vfo", h, ew[h][:], es[:, cols(h)], False)
-        prepare("bx", ["wex"])
-        for h in range(2):
-            product("b", "wex", h, xw[:, cols(h)], xs[:, cols(h)], True)
-        old = sb("old", [P, PICKS], F32)
-        nc.vector.tensor_copy(old[:], cell_sb[:].indirect(offs_sb[:]))
-        g = [sb("g0", [P, HALF], F32)[:], shared[:, cols(2)]]
-        f = shared[:, :PICKS]
+        prepare("b", ["wex", "vex"])
+        g = [raw["vex"][:, cols(0)], staged["b"][:].bitcast(F32)[:, cols(0)]]
+        f = [raw["vex"][:, cols(1)], staged["b"][:].bitcast(F32)[:, cols(1)]]
         fresh = sb("fresh", [P, PICKS], F32)
         kept = sb("kept", [P, PICKS], F32)
         new = sb("new", [P, PICKS], F32)
         th = sb("th", [P, PICKS], F32)
         b = sb("b", [P, PICKS], F32)
-
-        def gates(h):
-            nc.scalar.activation(g[h], acc["g", h][:], ACT.Tanh)
-            nc.scalar.activation(f[:, cols(h)], acc["f", h][:], ACT.Sigmoid)
-
-        gates(0)
-        cast("be", ["vex"], "vex", "scalar")
-        gates(1)
-        nc.vector.scalar_tensor_tensor(fresh[:, cols(0)], f[:, cols(0)], 1.0, g[0], ALU.subtract, ALU.mult)
-        quantise("be", ["vex"])
         for h in range(2):
+            nc.scalar.activation(g[h], acc["g", h][:], ACT.Tanh)
+            nc.scalar.activation(f[h], acc["f", h][:], ACT.Sigmoid)
+        for h in range(2):
+            product("b", "wex", h, xw[:, cols(h)], xs[:, cols(h)], True)
             product("b", "vex", h, ew[h][:], es[:, cols(h)], False)
             nc.scalar.activation(b[:, cols(h)], acc["b", h][:], ACT.Sigmoid)
-        nc.vector.tensor_tensor(kept[:], old[:], f, ALU.mult)
-        nc.vector.scalar_tensor_tensor(fresh[:, cols(1)], f[:, cols(1)], 1.0, g[1], ALU.subtract, ALU.mult)
+        for h in range(2):
+            nc.vector.scalar_tensor_tensor(fresh[:, cols(h)], f[h], 1.0, g[h], ALU.subtract, ALU.mult)
+            nc.vector.tensor_tensor(kept[:, cols(h)], cell_sb[:].indirect(offs_sb[:, h * HALF // 16 : (h + 1) * HALF // 16]), f[h], ALU.mult)
         for h in range(2):
             nc.vector.tensor_tensor(new[:, cols(h)], kept[:, cols(h)], fresh[:, cols(h)], ALU.subtract)
             nc.scalar.activation(th[:, cols(h)], new[:, cols(h)], ACT.Tanh)

@@ -30,7 +30,7 @@ def tile_picked_zlstm_cifg_p_kernel(
         psum = ctx.enter_context(tc.psum_pool(name="psum", bufs=1))
 
         reuse = ctx.enter_context(tc.tile_pool(name="reuse", bufs=1))
-        places = {"raw_vfo": 0, "ew1": 0}
+        places = {"raw_vfo": 0, "ew1": 0, "cell_sb": 4096, "new": 4096}
 
         def sb(name, shape, dtype, tag=None):
             if name in places:
@@ -116,12 +116,12 @@ def tile_picked_zlstm_cifg_p_kernel(
         nc.sync.dma_start(offs_sb[:], offs)
         load_words(xw_tab, x_words)
         load_scales(nc.sync, xs_tab, x_scales, range(4))
-        load_scales(nc.gpsimd, es_tab, e_scales, range(1))
+        load_scales(nc.gpsimd, es_tab, e_scales, range(2))
         load_weight("wca", wca)
         load_weight("wfo", wfo)
         load_words(ew_tab, e_words)
         nc.sync.dma_start(tok_sb[:], tok)
-        load_scales(nc.sync, es_tab, e_scales, range(1, 4))
+        load_scales(nc.sync, es_tab, e_scales, range(2, 4))
         load_weight("vca", vca)
         load_weight("vfo", vfo)
         load_weight("wex", wex)
@@ -146,33 +146,33 @@ def tile_picked_zlstm_cifg_p_kernel(
         nc.vector.tensor_copy(xs[:], xs_tab[:].indirect(offs_sb[:]))
         prepare("x", ["wca", "wfo"])
         for h in range(2):
-            product("g", "wca", h, xw[:, cols(h)], xs[:, cols(h)], True)
             product("f", "wfo", h, xw[:, cols(h)], xs[:, cols(h)], True)
+            product("g", "wca", h, xw[:, cols(h)], xs[:, cols(h)], True)
         gather_ew(0)
         nc.vector.tensor_copy(es[:], es_tab[:].indirect(tok_sb[:]))
         prepare("e", ["vca", "vfo"])
         gather_ew(1)
         for h in range(2):
-            product("g", "vca", h, ew[h][:], es[:, cols(h)], False)
             product("f", "vfo", h, ew[h][:], es[:, cols(h)], False)
+            product("g", "vca", h, ew[h][:], es[:, cols(h)], False)
         prepare("b", ["wex", "vex"])
-        g = [raw["vex"][:, cols(0)], staged["b"][:].bitcast(F32)[:, cols(0)]]
-        f = [raw["vex"][:, cols(1)], staged["b"][:].bitcast(F32)[:, cols(1)]]
+        g = [sb(f"g{h}", [P, HALF], F32)[:] for h in range(2)]
+        f = [sb(f"f{h}", [P, HALF], F32)[:] for h in range(2)]
         fresh = sb("fresh", [P, PICKS], F32)
         kept = sb("kept", [P, PICKS], F32)
         new = sb("new", [P, PICKS], F32)
         th = sb("th", [P, PICKS], F32)
         b = sb("b", [P, PICKS], F32)
         for h in range(2):
-            nc.scalar.activation(g[h], acc["g", h][:], ACT.Tanh)
             nc.scalar.activation(f[h], acc["f", h][:], ACT.Sigmoid)
+            nc.scalar.activation(g[h], acc["g", h][:], ACT.Tanh)
         for h in range(2):
             product("b", "wex", h, xw[:, cols(h)], xs[:, cols(h)], True)
             product("b", "vex", h, ew[h][:], es[:, cols(h)], False)
             nc.scalar.activation(b[:, cols(h)], acc["b", h][:], ACT.Sigmoid)
         for h in range(2):
-            nc.vector.scalar_tensor_tensor(fresh[:, cols(h)], f[h], 1.0, g[h], ALU.subtract, ALU.mult)
             nc.vector.tensor_tensor(kept[:, cols(h)], cell_sb[:].indirect(offs_sb[:, h * HALF // 16 : (h + 1) * HALF // 16]), f[h], ALU.mult)
+            nc.vector.scalar_tensor_tensor(fresh[:, cols(h)], f[h], 1.0, g[h], ALU.subtract, ALU.mult)
         for h in range(2):
             nc.vector.tensor_tensor(new[:, cols(h)], kept[:, cols(h)], fresh[:, cols(h)], ALU.subtract)
             nc.scalar.activation(th[:, cols(h)], new[:, cols(h)], ACT.Tanh)

@@ -30,7 +30,7 @@ def tile_picked_zlstm_cifg_p_kernel(
         psum = ctx.enter_context(tc.psum_pool(name="psum", bufs=1))
 
         reuse = ctx.enter_context(tc.tile_pool(name="reuse", bufs=1))
-        places = {"raw_vfo": 0, "ew1": 0, "cell_sb": 4096, "new": 4096}
+        places = {"raw_vfo": 0, "ew1": 0}
 
         def sb(name, shape, dtype, tag=None):
             if name in places:
@@ -45,10 +45,10 @@ def tile_picked_zlstm_cifg_p_kernel(
         ew_tab = sb("ew_tab", [P, TABLE], I32)
         cell_sb = sb("cell_sb", [P, TABLE], F32)
 
-        def load_scales(queue, table, scales, quadrants):
+        def load_scales(queue, table, scales, quadrants, row=0):
             for q in quadrants:
                 queue.dma_start(
-                    out=table[32 * q : 32 * q + 4, :].bitcast(I32),
+                    out=table[32 * q + row : 32 * q + row + 4, :].bitcast(I32),
                     in_=scales[0, 4 * q : 4 * q + 4, :].bitcast(I32),
                 )
 
@@ -116,12 +116,12 @@ def tile_picked_zlstm_cifg_p_kernel(
         nc.sync.dma_start(offs_sb[:], offs)
         load_words(xw_tab, x_words)
         load_scales(nc.sync, xs_tab, x_scales, range(4))
-        load_scales(nc.gpsimd, es_tab, e_scales, range(2))
+        load_scales(nc.gpsimd, es_tab, e_scales, range(2), 4)
         load_weight("wca", wca)
         load_weight("wfo", wfo)
         load_words(ew_tab, e_words)
         nc.sync.dma_start(tok_sb[:], tok)
-        load_scales(nc.sync, es_tab, e_scales, range(2, 4))
+        load_scales(nc.sync, es_tab, e_scales, range(2, 4), 4)
         load_weight("vca", vca)
         load_weight("vfo", vfo)
         load_weight("wex", wex)
@@ -153,14 +153,13 @@ def tile_picked_zlstm_cifg_p_kernel(
         prepare("e", ["vca", "vfo"])
         gather_ew(1)
         for h in range(2):
-            product("f", "vfo", h, ew[h][:], es[:, cols(h)], False)
-            product("g", "vca", h, ew[h][:], es[:, cols(h)], False)
+            product("f", "vfo", h, ew[h][:], es[4:P, cols(h)], False)
+            product("g", "vca", h, ew[h][:], es[4:P, cols(h)], False)
         prepare("b", ["wex", "vex"])
         g = [sb(f"g{h}", [P, HALF], F32)[:] for h in range(2)]
         f = [sb(f"f{h}", [P, HALF], F32)[:] for h in range(2)]
         fresh = sb("fresh", [P, PICKS], F32)
         kept = sb("kept", [P, PICKS], F32)
-        new = sb("new", [P, PICKS], F32)
         th = sb("th", [P, PICKS], F32)
         b = sb("b", [P, PICKS], F32)
         for h in range(2):
@@ -168,15 +167,31 @@ def tile_picked_zlstm_cifg_p_kernel(
             nc.scalar.activation(g[h], acc["g", h][:], ACT.Tanh)
         for h in range(2):
             product("b", "wex", h, xw[:, cols(h)], xs[:, cols(h)], True)
-            product("b", "vex", h, ew[h][:], es[:, cols(h)], False)
+            product("b", "vex", h, ew[h][:], es[4:P, cols(h)], False)
             nc.scalar.activation(b[:, cols(h)], acc["b", h][:], ACT.Sigmoid)
-        for h in range(2):
+        pieces = [slice(0, HALF), slice(HALF, HALF + UNITS), slice(HALF + UNITS, PICKS)]
+
+        def keep_old(h):
             nc.vector.tensor_tensor(kept[:, cols(h)], cell_sb[:].indirect(offs_sb[:, h * HALF // 16 : (h + 1) * HALF // 16]), f[h], ALU.mult)
-            nc.vector.scalar_tensor_tensor(fresh[:, cols(h)], f[h], 1.0, g[h], ALU.subtract, ALU.mult)
-        for h in range(2):
-            nc.vector.tensor_tensor(new[:, cols(h)], kept[:, cols(h)], fresh[:, cols(h)], ALU.subtract)
-            nc.scalar.activation(th[:, cols(h)], new[:, cols(h)], ACT.Tanh)
-        for h in range(2):
-            res = sb(f"res{h}", [P, HALF], F32)
-            nc.vector.tensor_tensor(res[:], b[:, cols(h)], th[:, cols(h)], ALU.mult)
-            nc.sync.dma_start(out=out[:, cols(h)], in_=res[:])
+
+        def add_fresh(c):
+            h, part = c.start // HALF, slice(c.start % HALF, c.start % HALF + c.stop - c.start)
+            nc.vector.scalar_tensor_tensor(fresh[:, c], f[h][:, part], 1.0, g[h][:, part], ALU.subtract, ALU.mult)
+
+        def squash(c):
+            nc.vector.tensor_tensor(new[c.start][:], kept[:, c], fresh[:, c], ALU.subtract)
+            nc.scalar.activation(th[:, c], new[c.start][:], ACT.Tanh)
+
+        keep_old(0)
+        add_fresh(pieces[0])
+        keep_old(1)
+        new = {c.start: sb(f"new{c.start}", [P, c.stop - c.start], F32) for c in pieces}
+        squash(pieces[0])
+        add_fresh(pieces[1])
+        add_fresh(pieces[2])
+        squash(pieces[1])
+        squash(pieces[2])
+        for c in pieces:
+            res = sb(f"res{c.start}", [P, c.stop - c.start], F32)
+            nc.vector.tensor_tensor(res[:], b[:, c], th[:, c], ALU.mult)
+            nc.sync.dma_start(out=out[:, c], in_=res[:])

@@ -45,11 +45,11 @@ def tile_picked_zlstm_cifg_p_kernel(
         ew_tab = sb("ew_tab", [P, TABLE], I32)
         cell_sb = sb("cell_sb", [P, TABLE], F32)
 
-        def load_scales(queue, table, scales, quadrants, row=0):
-            for q in quadrants:
+        def load_scales(queue, table, scales, rows, first=0):
+            for r in rows:
                 queue.dma_start(
-                    out=table[32 * q + row : 32 * q + row + 4, :].bitcast(I32),
-                    in_=scales[0, 4 * q : 4 * q + 4, :].bitcast(I32),
+                    out=table[first + r : P : 32, :].bitcast(I32),
+                    in_=scales[0, r : 16 : 4, :].bitcast(I32),
                 )
 
         def load_words(table, words):

@@ -108,7 +108,7 @@ def tile_picked_zlstm_cifg_p_kernel(
             nc.gpsimd.tensor_copy(c[:], ap)
 
         nc.vector.memset(xs_tab[:].bitcast(I32), 0)
-        nc.gpsimd.memset(es_tab[:].bitcast(I32), 0)
+        nc.vector.memset(es_tab[:].bitcast(I32), 0)
         warm_in = sb("warm_in", [P, 1], F32)
         warm_out = sb("warm_out", [P, 1], F32)
         nc.vector.memset(warm_in[:], 0.0)
@@ -116,12 +116,11 @@ def tile_picked_zlstm_cifg_p_kernel(
         nc.sync.dma_start(offs_sb[:], offs)
         load_words(xw_tab, x_words)
         load_scales(nc.sync, xs_tab, x_scales, range(4))
-        load_scales(nc.gpsimd, es_tab, e_scales, range(2), 4)
         load_weight("wca", wca)
         load_weight("wfo", wfo)
         load_words(ew_tab, e_words)
         nc.sync.dma_start(tok_sb[:], tok)
-        load_scales(nc.sync, es_tab, e_scales, range(2, 4), 4)
+        load_scales(nc.sync, es_tab, e_scales, range(4), 4)
         load_weight("vca", vca)
         load_weight("vfo", vfo)
         load_weight("wex", wex)

@@ -28,14 +28,13 @@ def tile_picked_zlstm_cifg_p_kernel(
     with ExitStack() as ctx:
         keep = ctx.enter_context(tc.tile_pool(name="keep", bufs=1))
         psum = ctx.enter_context(tc.psum_pool(name="psum", bufs=1))
-
         reuse = ctx.enter_context(tc.tile_pool(name="reuse", bufs=1))
-        places = {"raw_vfo": 0, "ew1": 0}
+        places = {"f": 0, "raw_vex": 1984, "g": 3968, "cell_sb": 6144, "b": 6144}
 
-        def sb(name, shape, dtype, tag=None):
+        def sb(name, shape, dtype):
             if name in places:
                 return reuse.tile(shape, dtype, name=name, align_bytes=64, offset=places[name])
-            return keep.tile(shape, dtype, name=name, tag=tag or name, align_bytes=64)
+            return keep.tile(shape, dtype, name=name, align_bytes=64)
 
         offs_sb = keep.tile([P, PICKS // 16], U16, name="offs_sb")
         tok_sb = keep.tile([P, PICKS // 16], U16, name="tok_sb")
@@ -45,9 +44,9 @@ def tile_picked_zlstm_cifg_p_kernel(
         ew_tab = sb("ew_tab", [P, TABLE], I32)
         cell_sb = sb("cell_sb", [P, TABLE], F32)
 
-        def load_scales(queue, table, scales, rows, first=0):
-            for r in rows:
-                queue.dma_start(
+        def load_scales(table, scales, first):
+            for r in range(4):
+                nc.sync.dma_start(
                     out=table[first + r : P : 32, :].bitcast(I32),
                     in_=scales[0, r : 16 : 4, :].bitcast(I32),
                 )
@@ -63,24 +62,25 @@ def tile_picked_zlstm_cifg_p_kernel(
 
         codes, scales, staged = {}, {}, {}
 
-        def cast(group, names, name, engine):
-            if group not in staged:
-                staged[group] = sb("grouped_" + group, [P, len(names) * UNITS * PACK], BF16)
-            i = names.index(name)
-            dst = staged[group][:, i * UNITS * PACK : (i + 1) * UNITS * PACK].rearrange("p (c i t) -> p c t i", i=4, t=PACK)
+        def stage(group, names):
+            tile = sb("grouped_" + group, [P, len(names) * UNITS * PACK], BF16)
+            for i, name in enumerate(names):
+                staged[name] = tile[:, i * UNITS * PACK : (i + 1) * UNITS * PACK]
+            staged[group] = tile[:]
+
+        def cast(name, engine):
+            dst = staged[name].rearrange("p (c i t) -> p c t i", i=4, t=PACK)
             src = raw[name][:].rearrange("p (t c i) -> p c t i", t=PACK, i=4)
             if engine == "scalar":
                 nc.scalar.copy(out=dst, in_=src)
-            elif engine == "vector":
-                nc.vector.tensor_copy(out=dst, in_=src)
             else:
-                nc.gpsimd.tensor_copy(out=dst, in_=src)
+                nc.vector.tensor_copy(out=dst, in_=src)
 
         def quantise(group, names):
             n = len(names)
             cw = sb("codes_" + group, [P, n * UNITS], U32)
             cs = sb("scales_" + group, [P, n * UNITS], U8)
-            nc.vector.quantize_mx(out=cw[:].bitcast(FP8X4), scales=cs[:], in_=staged[group][:])
+            nc.vector.quantize_mx(out=cw[:].bitcast(FP8X4), scales=cs[:], in_=staged[group])
             for i, name in enumerate(names):
                 codes[name] = cw[:, i * UNITS : (i + 1) * UNITS]
                 scales[name] = cs[:, i * UNITS : (i + 1) * UNITS]
@@ -103,6 +103,9 @@ def tile_picked_zlstm_cifg_p_kernel(
         def cols(h):
             return slice(h * HALF, (h + 1) * HALF)
 
+        def entries(lst, h):
+            return lst[:, h * HALF // 16 : (h + 1) * HALF // 16]
+
         def clock(name, ap):
             c = sb("clock_" + name, [P, 1], ap.dtype)
             nc.gpsimd.tensor_copy(c[:], ap)
@@ -113,16 +116,17 @@ def tile_picked_zlstm_cifg_p_kernel(
         warm_out = sb("warm_out", [P, 1], F32)
         nc.vector.memset(warm_in[:], 0.0)
         nc.scalar.activation(warm_out[:], warm_in[:], ACT.Sigmoid)
+
         nc.sync.dma_start(offs_sb[:], offs)
-        load_words(xw_tab, x_words)
-        load_scales(nc.sync, xs_tab, x_scales, range(4))
         load_weight("wca", wca)
-        load_weight("wfo", wfo)
-        load_words(ew_tab, e_words)
+        load_scales(xs_tab, x_scales, 0)
         nc.sync.dma_start(tok_sb[:], tok)
-        load_scales(nc.sync, es_tab, e_scales, range(4), 4)
+        load_words(xw_tab, x_words)
+        load_weight("wfo", wfo)
+        load_scales(es_tab, e_scales, 4)
         load_weight("vca", vca)
         load_weight("vfo", vfo)
+        load_words(ew_tab, e_words)
         load_weight("wex", wex)
         load_weight("vex", vex)
         nc.sync.dma_start(out=cell_sb[:], in_=cell)
@@ -130,67 +134,75 @@ def tile_picked_zlstm_cifg_p_kernel(
         xs = sb("xs", [P, PICKS], U8)
         xw = sb("xw", [P, PICKS], U32)
         es = sb("es", [P, PICKS], U8)
-        ew = {}
+        ew = sb("ew", [P, PICKS], U32)
 
-        def prepare(group, names):
-            for name in names:
-                cast(group, names, name, "scalar")
-            quantise(group, names)
+        stage("x", ["wca", "wfo"])
+        stage("e", ["vca", "vfo"])
+        stage("b", ["wex", "vex"])
 
-        def gather_ew(h):
-            ew[h] = sb(f"ew{h}", [P, HALF], U32)
-            nc.vector.tensor_copy(ew[h][:], ew_tab[:].bitcast(U32).indirect(tok_sb[:, h * HALF // 16 : (h + 1) * HALF // 16]))
-
-        nc.vector.tensor_copy(xw[:], xw_tab[:].bitcast(U32).indirect(offs_sb[:]))
         nc.vector.tensor_copy(xs[:], xs_tab[:].indirect(offs_sb[:]))
-        prepare("x", ["wca", "wfo"])
+        cast("wca", "scalar")
+        nc.vector.tensor_copy(xw[:], xw_tab[:].bitcast(U32).indirect(offs_sb[:]))
+        cast("wfo", "scalar")
+        quantise("x", ["wca", "wfo"])
+        nc.vector.tensor_copy(es[:], es_tab[:].indirect(tok_sb[:]))
         for h in range(2):
             product("f", "wfo", h, xw[:, cols(h)], xs[:, cols(h)], True)
             product("g", "wca", h, xw[:, cols(h)], xs[:, cols(h)], True)
-        gather_ew(0)
-        nc.vector.tensor_copy(es[:], es_tab[:].indirect(tok_sb[:]))
-        prepare("e", ["vca", "vfo"])
-        gather_ew(1)
+        cast("vca", "scalar")
+        cast("vfo", "scalar")
+        quantise("e", ["vca", "vfo"])
         for h in range(2):
-            product("f", "vfo", h, ew[h][:], es[4:P, cols(h)], False)
-            product("g", "vca", h, ew[h][:], es[4:P, cols(h)], False)
-        prepare("b", ["wex", "vex"])
-        g = [sb(f"g{h}", [P, HALF], F32)[:] for h in range(2)]
-        f = [sb(f"f{h}", [P, HALF], F32)[:] for h in range(2)]
+            nc.vector.tensor_copy(ew[:, cols(h)], ew_tab[:].bitcast(U32).indirect(entries(tok_sb, h)))
+            product("f", "vfo", h, ew[:, cols(h)], es[4:P, cols(h)], False)
+            product("g", "vca", h, ew[:, cols(h)], es[4:P, cols(h)], False)
+        cast("wex", "scalar")
+        cast("vex", "scalar")
+        quantise("b", ["wex", "vex"])
+
+        g = sb("g", [P, PICKS], F32)
+        f = sb("f", [P, PICKS], F32)
+        b = sb("b", [P, PICKS], F32)
         fresh = sb("fresh", [P, PICKS], F32)
         kept = sb("kept", [P, PICKS], F32)
         th = sb("th", [P, PICKS], F32)
-        b = sb("b", [P, PICKS], F32)
+        old1 = sb("old1", [P, HALF], F32)
         for h in range(2):
-            nc.scalar.activation(f[h], acc["f", h][:], ACT.Sigmoid)
-            nc.scalar.activation(g[h], acc["g", h][:], ACT.Tanh)
-        for h in range(2):
-            product("b", "wex", h, xw[:, cols(h)], xs[:, cols(h)], True)
-            product("b", "vex", h, ew[h][:], es[4:P, cols(h)], False)
-            nc.scalar.activation(b[:, cols(h)], acc["b", h][:], ACT.Sigmoid)
+            nc.scalar.activation(f[:, cols(h)], acc["f", h][:], ACT.Sigmoid)
+            nc.scalar.activation(g[:, cols(h)], acc["g", h][:], ACT.Tanh)
+        acc_b = psum.tile([P, PICKS], F32, name="acc_b")
+        for name, words, bytes_, first in (("wex", xw, xs[:], True), ("vex", ew, es[4:P, :], False)):
+            nc.tensor.matmul_mx(
+                out=acc_b[:],
+                lhsT=codes[name].bitcast(FP8X4),
+                lhsT_scale=scales[name],
+                rhs=words[:].bitcast(FP8X4),
+                rhs_scale=bytes_,
+                start=first,
+                stop=not first,
+            )
+
+        def make_fresh(h):
+            nc.vector.scalar_tensor_tensor(fresh[:, cols(h)], f[:, cols(h)], 1.0, g[:, cols(h)], ALU.subtract, ALU.mult)
+
         pieces = [slice(0, HALF), slice(HALF, HALF + UNITS), slice(HALF + UNITS, PICKS)]
+        new = [sb(f"new{i}", [P, c.stop - c.start], F32) for i, c in enumerate(pieces)]
+        res = [sb(f"res{i}", [P, c.stop - c.start], F32) for i, c in enumerate(pieces)]
 
-        def keep_old(h):
-            nc.vector.tensor_tensor(kept[:, cols(h)], cell_sb[:].indirect(offs_sb[:, h * HALF // 16 : (h + 1) * HALF // 16]), f[h], ALU.mult)
+        def add_up(i):
+            nc.vector.tensor_tensor(new[i][:], kept[:, pieces[i]], fresh[:, pieces[i]], ALU.subtract)
 
-        def add_fresh(c):
-            h, part = c.start // HALF, slice(c.start % HALF, c.start % HALF + c.stop - c.start)
-            nc.vector.scalar_tensor_tensor(fresh[:, c], f[h][:, part], 1.0, g[h][:, part], ALU.subtract, ALU.mult)
-
-        def squash(c):
-            nc.vector.tensor_tensor(new[c.start][:], kept[:, c], fresh[:, c], ALU.subtract)
-            nc.scalar.activation(th[:, c], new[c.start][:], ACT.Tanh)
-
-        keep_old(0)
-        add_fresh(pieces[0])
-        keep_old(1)
-        new = {c.start: sb(f"new{c.start}", [P, c.stop - c.start], F32) for c in pieces}
-        squash(pieces[0])
-        add_fresh(pieces[1])
-        add_fresh(pieces[2])
-        squash(pieces[1])
-        squash(pieces[2])
-        for c in pieces:
-            res = sb(f"res{c.start}", [P, c.stop - c.start], F32)
-            nc.vector.tensor_tensor(res[:], b[:, c], th[:, c], ALU.mult)
-            nc.sync.dma_start(out=out[:, c], in_=res[:])
+        nc.vector.tensor_tensor(kept[:, cols(0)], cell_sb[:].indirect(entries(offs_sb, 0)), f[:, cols(0)], ALU.mult)
+        nc.scalar.activation(old1[:], cell_sb[:].indirect(entries(offs_sb, 1)), ACT.Copy)
+        make_fresh(0)
+        make_fresh(1)
+        add_up(0)
+        nc.vector.tensor_tensor(kept[:, cols(1)], old1[:], f[:, cols(1)], ALU.mult)
+        nc.scalar.activation(b[:], acc_b[:], ACT.Sigmoid)
+        add_up(1)
+        add_up(2)
+        for i, c in enumerate(pieces):
+            nc.scalar.activation(th[:, c], new[i][:], ACT.Tanh)
+        for i, c in enumerate(pieces):
+            nc.vector.tensor_tensor(res[i][:], b[:, c], th[:, c], ALU.mult)
+            nc.sync.dma_start(out=out[:, c], in_=res[i][:])

@@ -29,7 +29,10 @@ def tile_picked_zlstm_cifg_p_kernel(
         keep = ctx.enter_context(tc.tile_pool(name="keep", bufs=1))
         psum = ctx.enter_context(tc.psum_pool(name="psum", bufs=1))
         reuse = ctx.enter_context(tc.tile_pool(name="reuse", bufs=1))
-        places = {"f": 0, "raw_vex": 1984, "g": 3968, "cell_sb": 6144, "b": 6144}
+        places = {
+            "raw_wex": 1984, "xs_tab": 2048, "es1": 2048, "f": 4160, "g": 8128,
+            "raw_vex": 6144, "ew_tab": 8128, "cell_sb": 12160,
+        }
 
         def sb(name, shape, dtype):
             if name in places:
@@ -49,6 +52,13 @@ def tile_picked_zlstm_cifg_p_kernel(
                 nc.sync.dma_start(
                     out=table[first + r : P : 32, :].bitcast(I32),
                     in_=scales[0, r : 16 : 4, :].bitcast(I32),
+                )
+
+        def place_scales(plane, picked, first):
+            for r in range(4):
+                nc.sync.dma_start(
+                    out=plane[first + r : P : 32, :].bitcast(I32),
+                    in_=picked[first + 8 * r : P : 32, :].bitcast(I32),
                 )
 
         def load_words(table, words):
@@ -110,99 +120,110 @@ def tile_picked_zlstm_cifg_p_kernel(
             c = sb("clock_" + name, [P, 1], ap.dtype)
             nc.gpsimd.tensor_copy(c[:], ap)
 
-        nc.vector.memset(xs_tab[:].bitcast(I32), 0)
-        nc.vector.memset(es_tab[:].bitcast(I32), 0)
+        xs_picked = sb("xs_picked", [P, PICKS], U8)
+        xs = sb("xs", [P, PICKS], U8)
+        es = [sb(f"es{h}", [P, HALF], U8) for h in range(2)]
+        xw = sb("xw", [P, PICKS], U32)
+        ew = sb("ew", [P, PICKS], U32)
+        for plane in (xs_tab, es_tab):
+            nc.vector.memset(plane[:].bitcast(I32), 0)
         warm_in = sb("warm_in", [P, 1], F32)
         warm_out = sb("warm_out", [P, 1], F32)
         nc.vector.memset(warm_in[:], 0.0)
-        nc.scalar.activation(warm_out[:], warm_in[:], ACT.Sigmoid)
+        nc.vector.memset(xs[:].bitcast(I32), 0)
 
         nc.sync.dma_start(offs_sb[:], offs)
-        load_weight("wca", wca)
-        load_scales(xs_tab, x_scales, 0)
-        nc.sync.dma_start(tok_sb[:], tok)
-        load_words(xw_tab, x_words)
-        load_weight("wfo", wfo)
-        load_scales(es_tab, e_scales, 4)
         load_weight("vca", vca)
-        load_weight("vfo", vfo)
+        nc.sync.dma_start(out=xs_tab[0:P:8, :].bitcast(I32), in_=x_scales[0].bitcast(I32))
+        nc.sync.dma_start(tok_sb[:], tok)
+        nc.scalar.activation(warm_out[:], warm_in[:], ACT.Sigmoid)
         load_words(ew_tab, e_words)
+        load_weight("vfo", vfo)
+        load_scales(es_tab, e_scales, 4)
+        load_weight("wca", wca)
+        load_weight("wfo", wfo)
+        load_words(xw_tab, x_words)
+
+        nc.vector.tensor_copy(xs_picked[:], xs_tab[:].indirect(offs_sb[:]))
+        place_scales(xs, xs_picked, 0)
         load_weight("wex", wex)
         load_weight("vex", vex)
         nc.sync.dma_start(out=cell_sb[:], in_=cell)
 
-        xs = sb("xs", [P, PICKS], U8)
-        xw = sb("xw", [P, PICKS], U32)
-        es = sb("es", [P, PICKS], U8)
-        ew = sb("ew", [P, PICKS], U32)
-
-        stage("x", ["wca", "wfo"])
         stage("e", ["vca", "vfo"])
         stage("b", ["wex", "vex"])
+        stage("x", ["wca", "wfo"])
 
-        nc.vector.tensor_copy(xs[:], xs_tab[:].indirect(offs_sb[:]))
-        cast("wca", "scalar")
-        nc.vector.tensor_copy(xw[:], xw_tab[:].bitcast(U32).indirect(offs_sb[:]))
-        cast("wfo", "scalar")
-        quantise("x", ["wca", "wfo"])
-        nc.vector.tensor_copy(es[:], es_tab[:].indirect(tok_sb[:]))
-        for h in range(2):
-            product("f", "wfo", h, xw[:, cols(h)], xs[:, cols(h)], True)
-            product("g", "wca", h, xw[:, cols(h)], xs[:, cols(h)], True)
+        def gather_es(h):
+            nc.vector.tensor_copy(es[h][:], es_tab[:].indirect(entries(tok_sb, h)))
+
+        def state_pass(gate, name, h, first):
+            product(gate, name, h, xw[:, cols(h)], xs[:, cols(h)], first)
+
+        def token_pass(gate, name, h, first):
+            product(gate, name, h, ew[:, cols(h)], es[h][4:P, :], first)
+
         cast("vca", "scalar")
         cast("vfo", "scalar")
+        nc.vector.tensor_copy(ew[:], ew_tab[:].bitcast(U32).indirect(tok_sb[:]))
+        gather_es(0)
         quantise("e", ["vca", "vfo"])
+        token_pass("f", "vfo", 0, True)
+        token_pass("g", "vca", 0, True)
+        cast("wca", "scalar")
+        cast("wfo", "scalar")
+        quantise("x", ["wca", "wfo"])
         for h in range(2):
-            nc.vector.tensor_copy(ew[:, cols(h)], ew_tab[:].bitcast(U32).indirect(entries(tok_sb, h)))
-            product("f", "vfo", h, ew[:, cols(h)], es[4:P, cols(h)], False)
-            product("g", "vca", h, ew[:, cols(h)], es[4:P, cols(h)], False)
+            nc.vector.tensor_copy(xw[:, cols(h)], xw_tab[:].bitcast(U32).indirect(entries(offs_sb, h)))
+        state_pass("f", "wfo", 0, False)
+        state_pass("g", "wca", 0, False)
+        state_pass("f", "wfo", 1, True)
+        state_pass("g", "wca", 1, True)
         cast("wex", "scalar")
+        gather_es(1)
+        token_pass("f", "vfo", 1, False)
+        token_pass("g", "vca", 1, False)
         cast("vex", "scalar")
         quantise("b", ["wex", "vex"])
 
         g = sb("g", [P, PICKS], F32)
         f = sb("f", [P, PICKS], F32)
         b = sb("b", [P, PICKS], F32)
-        fresh = sb("fresh", [P, PICKS], F32)
-        kept = sb("kept", [P, PICKS], F32)
         th = sb("th", [P, PICKS], F32)
-        old1 = sb("old1", [P, HALF], F32)
+        kept = sb("kept", [P, PICKS], F32)
+        fresh = sb("fresh", [P, PICKS], F32)
         for h in range(2):
             nc.scalar.activation(f[:, cols(h)], acc["f", h][:], ACT.Sigmoid)
             nc.scalar.activation(g[:, cols(h)], acc["g", h][:], ACT.Tanh)
-        acc_b = psum.tile([P, PICKS], F32, name="acc_b")
-        for name, words, bytes_, first in (("wex", xw, xs[:], True), ("vex", ew, es[4:P, :], False)):
-            nc.tensor.matmul_mx(
-                out=acc_b[:],
-                lhsT=codes[name].bitcast(FP8X4),
-                lhsT_scale=scales[name],
-                rhs=words[:].bitcast(FP8X4),
-                rhs_scale=bytes_,
-                start=first,
-                stop=not first,
-            )
-
-        def make_fresh(h):
-            nc.vector.scalar_tensor_tensor(fresh[:, cols(h)], f[:, cols(h)], 1.0, g[:, cols(h)], ALU.subtract, ALU.mult)
+        for h in range(2):
+            state_pass("b", "wex", h, True)
+            token_pass("b", "vex", h, False)
+            nc.scalar.activation(b[:, cols(h)], acc["b", h][:], ACT.Sigmoid)
 
         pieces = [slice(0, HALF), slice(HALF, HALF + UNITS), slice(HALF + UNITS, PICKS)]
         new = [sb(f"new{i}", [P, c.stop - c.start], F32) for i, c in enumerate(pieces)]
         res = [sb(f"res{i}", [P, c.stop - c.start], F32) for i, c in enumerate(pieces)]
 
-        def add_up(i):
-            nc.vector.tensor_tensor(new[i][:], kept[:, pieces[i]], fresh[:, pieces[i]], ALU.subtract)
+        def keep_old(h):
+            nc.vector.tensor_tensor(kept[:, cols(h)], cell_sb[:].indirect(entries(offs_sb, h)), f[:, cols(h)], ALU.mult)
 
-        nc.vector.tensor_tensor(kept[:, cols(0)], cell_sb[:].indirect(entries(offs_sb, 0)), f[:, cols(0)], ALU.mult)
-        nc.scalar.activation(old1[:], cell_sb[:].indirect(entries(offs_sb, 1)), ACT.Copy)
-        make_fresh(0)
-        make_fresh(1)
-        add_up(0)
-        nc.vector.tensor_tensor(kept[:, cols(1)], old1[:], f[:, cols(1)], ALU.mult)
-        nc.scalar.activation(b[:], acc_b[:], ACT.Sigmoid)
-        add_up(1)
-        add_up(2)
-        for i, c in enumerate(pieces):
+        def make_fresh(i):
+            c = pieces[i]
+            nc.vector.scalar_tensor_tensor(fresh[:, c], f[:, c], 1.0, g[:, c], ALU.subtract, ALU.mult)
+
+        def make_new(i):
+            c = pieces[i]
+            nc.vector.tensor_tensor(new[i][:], kept[:, c], fresh[:, c], ALU.subtract)
             nc.scalar.activation(th[:, c], new[i][:], ACT.Tanh)
+
+        keep_old(0)
+        make_fresh(0)
+        keep_old(1)
+        make_new(0)
+        make_fresh(1)
+        make_fresh(2)
+        make_new(1)
+        make_new(2)
         for i, c in enumerate(pieces):
             nc.vector.tensor_tensor(res[i][:], b[:, c], th[:, c], ALU.mult)
             nc.sync.dma_start(out=out[:, c], in_=res[i][:])

@@ -18,6 +18,7 @@ TABLE = 1024
 PICKS = 512
 UNITS = 128
 HALF = 256
+EARLY = 384
 FLOPS = 2 * 6 * 512 * UNITS * PICKS
 
 
@@ -30,7 +31,7 @@ def tile_picked_zlstm_cifg_p_kernel(
         psum = ctx.enter_context(tc.psum_pool(name="psum", bufs=1))
         reuse = ctx.enter_context(tc.tile_pool(name="reuse", bufs=1))
         places = {
-            "raw_wex": 1984, "xs_tab": 2048, "es1": 2048, "f": 4160, "g": 8128,
+            "raw_wex": 1984, "xs_tab": 2048, "es_late": 2048, "f0": 5184, "g0": 8128, "f1": 12160, "g1": 13184, "b": 14208,
             "raw_vex": 6144, "ew_tab": 8128, "cell_sb": 12160,
         }
 
@@ -78,9 +79,9 @@ def tile_picked_zlstm_cifg_p_kernel(
                 staged[name] = tile[:, i * UNITS * PACK : (i + 1) * UNITS * PACK]
             staged[group] = tile[:]
 
-        def cast(name, engine):
-            dst = staged[name].rearrange("p (c i t) -> p c t i", i=4, t=PACK)
-            src = raw[name][:].rearrange("p (t c i) -> p c t i", t=PACK, i=4)
+        def cast(name, engine, part=slice(0, UNITS // 4)):
+            dst = staged[name].rearrange("p (c i t) -> p c t i", i=4, t=PACK)[:, part]
+            src = raw[name][:].rearrange("p (t c i) -> p c t i", t=PACK, i=4)[:, part]
             if engine == "scalar":
                 nc.scalar.copy(out=dst, in_=src)
             else:
@@ -97,17 +98,17 @@ def tile_picked_zlstm_cifg_p_kernel(
 
         acc = {}
 
-        def product(gate, name, h, words, bytes_, first):
+        def product(gate, name, h, part, words, bytes_, first, last):
             if first:
                 acc[gate, h] = psum.tile([P, HALF], F32, name=f"acc_{gate}{h}")
             nc.tensor.matmul_mx(
-                out=acc[gate, h][:],
+                out=acc[gate, h][:, part],
                 lhsT=codes[name].bitcast(FP8X4),
                 lhsT_scale=scales[name],
                 rhs=words.bitcast(FP8X4),
                 rhs_scale=bytes_,
                 start=first,
-                stop=not first,
+                stop=last,
             )
 
         def cols(h):
@@ -122,7 +123,8 @@ def tile_picked_zlstm_cifg_p_kernel(
 
         xs_picked = sb("xs_picked", [P, PICKS], U8)
         xs = sb("xs", [P, PICKS], U8)
-        es = [sb(f"es{h}", [P, HALF], U8) for h in range(2)]
+        es_early = sb("es_early", [P, EARLY], U8)
+        es_late = sb("es_late", [P, PICKS - EARLY], U8)
         xw = sb("xw", [P, PICKS], U32)
         ew = sb("ew", [P, PICKS], U32)
         for plane in (xs_tab, es_tab):
@@ -154,19 +156,20 @@ def tile_picked_zlstm_cifg_p_kernel(
         stage("b", ["wex", "vex"])
         stage("x", ["wca", "wfo"])
 
-        def gather_es(h):
-            nc.vector.tensor_copy(es[h][:], es_tab[:].indirect(entries(tok_sb, h)))
-
         def state_pass(gate, name, h, first):
-            product(gate, name, h, xw[:, cols(h)], xs[:, cols(h)], first)
+            product(gate, name, h, slice(0, HALF), xw[:, cols(h)], xs[:, cols(h)], first, not first)
 
         def token_pass(gate, name, h, first):
-            product(gate, name, h, ew[:, cols(h)], es[h][4:P, :], first)
+            if h == 0:
+                product(gate, name, h, slice(0, HALF), ew[:, cols(h)], es_early[4:P, cols(h)], first, not first)
+            else:
+                product(gate, name, h, slice(0, EARLY - HALF), ew[:, HALF:EARLY], es_early[4:P, HALF:EARLY], False, False)
+                product(gate, name, h, slice(EARLY - HALF, HALF), ew[:, EARLY:PICKS], es_late[4:P, :], False, True)
 
         cast("vca", "scalar")
         cast("vfo", "scalar")
         nc.vector.tensor_copy(ew[:], ew_tab[:].bitcast(U32).indirect(tok_sb[:]))
-        gather_es(0)
+        nc.vector.tensor_copy(es_early[:], es_tab[:].indirect(tok_sb[:, 0 : EARLY // 16]))
         quantise("e", ["vca", "vfo"])
         token_pass("f", "vfo", 0, True)
         token_pass("g", "vca", 0, True)
@@ -180,46 +183,51 @@ def tile_picked_zlstm_cifg_p_kernel(
         state_pass("f", "wfo", 1, True)
         state_pass("g", "wca", 1, True)
         cast("wex", "scalar")
-        gather_es(1)
+        cast("vex", "vector", slice(0, UNITS // 16))
+        cast("vex", "scalar", slice(UNITS // 16, UNITS // 4))
+        nc.vector.tensor_copy(es_late[:], es_tab[:].indirect(tok_sb[:, EARLY // 16 : PICKS // 16]))
         token_pass("f", "vfo", 1, False)
         token_pass("g", "vca", 1, False)
-        cast("vex", "scalar")
         quantise("b", ["wex", "vex"])
 
-        g = sb("g", [P, PICKS], F32)
-        f = sb("f", [P, PICKS], F32)
+        g = [sb(f"g{h}", [P, HALF], F32) for h in range(2)]
+        f = [sb(f"f{h}", [P, HALF], F32) for h in range(2)]
         b = sb("b", [P, PICKS], F32)
         th = sb("th", [P, PICKS], F32)
         kept = sb("kept", [P, PICKS], F32)
         fresh = sb("fresh", [P, PICKS], F32)
-        for h in range(2):
-            nc.scalar.activation(f[:, cols(h)], acc["f", h][:], ACT.Sigmoid)
-            nc.scalar.activation(g[:, cols(h)], acc["g", h][:], ACT.Tanh)
-        for h in range(2):
-            state_pass("b", "wex", h, True)
-            token_pass("b", "vex", h, False)
-            nc.scalar.activation(b[:, cols(h)], acc["b", h][:], ACT.Sigmoid)
+        old = sb("old", [P, HALF], F32)
+
+        def gates(h):
+            nc.scalar.activation(f[h][:], acc["f", h][:], ACT.Sigmoid)
+            nc.scalar.activation(g[h][:], acc["g", h][:], ACT.Tanh)
+
+        gates(0)
+        nc.scalar.activation(old[:], cell_sb[:].indirect(entries(offs_sb, 1)), ACT.Copy)
 
         pieces = [slice(0, HALF), slice(HALF, HALF + UNITS), slice(HALF + UNITS, PICKS)]
         new = [sb(f"new{i}", [P, c.stop - c.start], F32) for i, c in enumerate(pieces)]
         res = [sb(f"res{i}", [P, c.stop - c.start], F32) for i, c in enumerate(pieces)]
 
-        def keep_old(h):
-            nc.vector.tensor_tensor(kept[:, cols(h)], cell_sb[:].indirect(entries(offs_sb, h)), f[:, cols(h)], ALU.mult)
-
         def make_fresh(i):
             c = pieces[i]
-            nc.vector.scalar_tensor_tensor(fresh[:, c], f[:, c], 1.0, g[:, c], ALU.subtract, ALU.mult)
+            h, part = c.start // HALF, slice(c.start % HALF, c.start % HALF + c.stop - c.start)
+            nc.vector.scalar_tensor_tensor(fresh[:, c], f[h][:, part], 1.0, g[h][:, part], ALU.subtract, ALU.mult)
 
         def make_new(i):
             c = pieces[i]
             nc.vector.tensor_tensor(new[i][:], kept[:, c], fresh[:, c], ALU.subtract)
             nc.scalar.activation(th[:, c], new[i][:], ACT.Tanh)
 
-        keep_old(0)
+        nc.vector.tensor_tensor(kept[:, cols(0)], cell_sb[:].indirect(entries(offs_sb, 0)), f[0][:], ALU.mult)
+        gates(1)
+        for h in range(2):
+            state_pass("b", "wex", h, True)
+            token_pass("b", "vex", h, False)
+            nc.scalar.activation(b[:, cols(h)], acc["b", h][:], ACT.Sigmoid)
         make_fresh(0)
-        keep_old(1)
         make_new(0)
+        nc.vector.tensor_tensor(kept[:, cols(1)], old[:], f[1][:], ALU.mult)
         make_fresh(1)
         make_fresh(2)
         make_new(1)

@@ -18,7 +18,6 @@ TABLE = 1024
 PICKS = 512
 UNITS = 128
 HALF = 256
-EARLY = 384
 FLOPS = 2 * 6 * 512 * UNITS * PICKS
 
 
@@ -31,7 +30,7 @@ def tile_picked_zlstm_cifg_p_kernel(
         psum = ctx.enter_context(tc.psum_pool(name="psum", bufs=1))
         reuse = ctx.enter_context(tc.tile_pool(name="reuse", bufs=1))
         places = {
-            "raw_wex": 1984, "xs_tab": 2048, "es_late": 2048, "f0": 5184, "g0": 8128, "f1": 12160, "g1": 13184, "b": 14208,
+            "raw_wex": 1984, "xs_tab": 2048, "f0": 5184, "g0": 8128, "f1": 6208, "grouped_b": 16384, "g1": 16384, "b": 14208,
             "raw_vex": 6144, "ew_tab": 8128, "cell_sb": 12160,
         }
 
@@ -98,17 +97,17 @@ def tile_picked_zlstm_cifg_p_kernel(
 
         acc = {}
 
-        def product(gate, name, h, part, words, bytes_, first, last):
+        def product(gate, name, h, words, bytes_, first):
             if first:
                 acc[gate, h] = psum.tile([P, HALF], F32, name=f"acc_{gate}{h}")
             nc.tensor.matmul_mx(
-                out=acc[gate, h][:, part],
+                out=acc[gate, h][:],
                 lhsT=codes[name].bitcast(FP8X4),
                 lhsT_scale=scales[name],
                 rhs=words.bitcast(FP8X4),
                 rhs_scale=bytes_,
                 start=first,
-                stop=last,
+                stop=not first,
             )
 
         def cols(h):
@@ -123,8 +122,7 @@ def tile_picked_zlstm_cifg_p_kernel(
 
         xs_picked = sb("xs_picked", [P, PICKS], U8)
         xs = sb("xs", [P, PICKS], U8)
-        es_early = sb("es_early", [P, EARLY], U8)
-        es_late = sb("es_late", [P, PICKS - EARLY], U8)
+        es = sb("es", [P, PICKS], U8)
         xw = sb("xw", [P, PICKS], U32)
         ew = sb("ew", [P, PICKS], U32)
         for plane in (xs_tab, es_tab):
@@ -134,9 +132,9 @@ def tile_picked_zlstm_cifg_p_kernel(
         nc.vector.memset(warm_in[:], 0.0)
         nc.vector.memset(xs[:].bitcast(I32), 0)
 
-        nc.sync.dma_start(offs_sb[:], offs)
         load_weight("vca", vca)
-        nc.sync.dma_start(out=xs_tab[0:P:8, :].bitcast(I32), in_=x_scales[0].bitcast(I32))
+        nc.sync.dma_start(offs_sb[:], offs)
+        nc.scalar.dma_start(out=xs_tab[0:P:8, :].bitcast(I32), in_=x_scales[0].bitcast(I32))
         nc.sync.dma_start(tok_sb[:], tok)
         nc.scalar.activation(warm_out[:], warm_in[:], ACT.Sigmoid)
         load_words(ew_tab, e_words)
@@ -157,37 +155,29 @@ def tile_picked_zlstm_cifg_p_kernel(
         stage("x", ["wca", "wfo"])
 
         def state_pass(gate, name, h, first):
-            product(gate, name, h, slice(0, HALF), xw[:, cols(h)], xs[:, cols(h)], first, not first)
+            product(gate, name, h, xw[:, cols(h)], xs[:, cols(h)], first)
 
         def token_pass(gate, name, h, first):
-            if h == 0:
-                product(gate, name, h, slice(0, HALF), ew[:, cols(h)], es_early[4:P, cols(h)], first, not first)
-            else:
-                product(gate, name, h, slice(0, EARLY - HALF), ew[:, HALF:EARLY], es_early[4:P, HALF:EARLY], False, False)
-                product(gate, name, h, slice(EARLY - HALF, HALF), ew[:, EARLY:PICKS], es_late[4:P, :], False, True)
+            product(gate, name, h, ew[:, cols(h)], es[4:P, cols(h)], first)
 
         cast("vca", "scalar")
         cast("vfo", "scalar")
         nc.vector.tensor_copy(ew[:], ew_tab[:].bitcast(U32).indirect(tok_sb[:]))
-        nc.vector.tensor_copy(es_early[:], es_tab[:].indirect(tok_sb[:, 0 : EARLY // 16]))
         quantise("e", ["vca", "vfo"])
-        token_pass("f", "vfo", 0, True)
-        token_pass("g", "vca", 0, True)
+        for h in range(2):
+            nc.vector.tensor_copy(es[:, cols(h)], es_tab[:].indirect(entries(tok_sb, h)))
+            token_pass("f", "vfo", h, True)
+            token_pass("g", "vca", h, True)
         cast("wca", "scalar")
         cast("wfo", "scalar")
         quantise("x", ["wca", "wfo"])
         for h in range(2):
             nc.vector.tensor_copy(xw[:, cols(h)], xw_tab[:].bitcast(U32).indirect(entries(offs_sb, h)))
-        state_pass("f", "wfo", 0, False)
-        state_pass("g", "wca", 0, False)
-        state_pass("f", "wfo", 1, True)
-        state_pass("g", "wca", 1, True)
+            state_pass("f", "wfo", h, False)
+            state_pass("g", "wca", h, False)
         cast("wex", "scalar")
-        cast("vex", "vector", slice(0, UNITS // 16))
-        cast("vex", "scalar", slice(UNITS // 16, UNITS // 4))
-        nc.vector.tensor_copy(es_late[:], es_tab[:].indirect(tok_sb[:, EARLY // 16 : PICKS // 16]))
-        token_pass("f", "vfo", 1, False)
-        token_pass("g", "vca", 1, False)
+        cast("vex", "vector", slice(0, UNITS // 8))
+        cast("vex", "scalar", slice(UNITS // 8, UNITS // 4))
         quantise("b", ["wex", "vex"])
 
         g = [sb(f"g{h}", [P, HALF], F32) for h in range(2)]
@@ -198,21 +188,22 @@ def tile_picked_zlstm_cifg_p_kernel(
         fresh = sb("fresh", [P, PICKS], F32)
         old = sb("old", [P, HALF], F32)
 
-        def gates(h):
-            nc.scalar.activation(f[h][:], acc["f", h][:], ACT.Sigmoid)
-            nc.scalar.activation(g[h][:], acc["g", h][:], ACT.Tanh)
-
-        gates(0)
+        nc.scalar.activation(f[0][:], acc["f", 0][:], ACT.Sigmoid)
+        nc.scalar.activation(g[0][:], acc["g", 0][:], ACT.Tanh)
+        nc.scalar.activation(f[1][:], acc["f", 1][:], ACT.Sigmoid)
+        nc.scalar.activation(g[1][:], acc["g", 1][:], ACT.Tanh)
         nc.scalar.activation(old[:], cell_sb[:].indirect(entries(offs_sb, 1)), ACT.Copy)
 
         pieces = [slice(0, HALF), slice(HALF, HALF + UNITS), slice(HALF + UNITS, PICKS)]
         new = [sb(f"new{i}", [P, c.stop - c.start], F32) for i, c in enumerate(pieces)]
         res = [sb(f"res{i}", [P, c.stop - c.start], F32) for i, c in enumerate(pieces)]
 
-        def make_fresh(i):
-            c = pieces[i]
-            h, part = c.start // HALF, slice(c.start % HALF, c.start % HALF + c.stop - c.start)
-            nc.vector.scalar_tensor_tensor(fresh[:, c], f[h][:, part], 1.0, g[h][:, part], ALU.subtract, ALU.mult)
+        def make_fresh(h):
+            nc.vector.scalar_tensor_tensor(fresh[:, cols(h)], f[h][:], 1.0, g[h][:], ALU.subtract, ALU.mult)
+
+        def make_kept(i):
+            part = slice(pieces[i].start - HALF, pieces[i].stop - HALF)
+            nc.vector.tensor_tensor(kept[:, pieces[i]], old[:, part], f[1][:, part], ALU.mult)
 
         def make_new(i):
             c = pieces[i]
@@ -220,16 +211,15 @@ def tile_picked_zlstm_cifg_p_kernel(
             nc.scalar.activation(th[:, c], new[i][:], ACT.Tanh)
 
         nc.vector.tensor_tensor(kept[:, cols(0)], cell_sb[:].indirect(entries(offs_sb, 0)), f[0][:], ALU.mult)
-        gates(1)
         for h in range(2):
             state_pass("b", "wex", h, True)
             token_pass("b", "vex", h, False)
             nc.scalar.activation(b[:, cols(h)], acc["b", h][:], ACT.Sigmoid)
         make_fresh(0)
-        make_new(0)
-        nc.vector.tensor_tensor(kept[:, cols(1)], old[:], f[1][:], ALU.mult)
         make_fresh(1)
-        make_fresh(2)
+        make_new(0)
+        make_kept(1)
+        make_kept(2)
         make_new(1)
         make_new(2)
         for i, c in enumerate(pieces):

@@ -18,6 +18,7 @@ TABLE = 1024
 PICKS = 512
 UNITS = 128
 HALF = 256
+STAGE = 112
 FLOPS = 2 * 6 * 512 * UNITS * PICKS
 
 
@@ -30,8 +31,9 @@ def tile_picked_zlstm_cifg_p_kernel(
         psum = ctx.enter_context(tc.psum_pool(name="psum", bufs=1))
         reuse = ctx.enter_context(tc.tile_pool(name="reuse", bufs=1))
         places = {
-            "raw_wex": 1984, "xs_tab": 2048, "f0": 5184, "g0": 8128, "f1": 6208, "grouped_b": 16384, "g1": 16384, "b": 14208,
-            "raw_vex": 6144, "ew_tab": 8128, "cell_sb": 12160,
+            "raw_wex": 1984, "xs_tab": 2048, "raw_vex": 6144, "ew_tab": 8128, "cell_sb": 12160, "b": 14208,
+            "f0": 1024, "f1": 2048, "g0": 3072, "kept1": 3072, "grouped_b": 24576, "g1": 24576,
+            "codes_x": 16384, "old": 16384, "xw0": 20480, "fresh": 20480,
         }
 
         def sb(name, shape, dtype):
@@ -58,7 +60,7 @@ def tile_picked_zlstm_cifg_p_kernel(
             for r in range(4):
                 nc.sync.dma_start(
                     out=plane[first + r : P : 32, :].bitcast(I32),
-                    in_=picked[first + 8 * r : P : 32, :].bitcast(I32),
+                    in_=picked[STAGE + r : P : 4, :].bitcast(I32),
                 )
 
         def load_words(table, words):
@@ -83,6 +85,12 @@ def tile_picked_zlstm_cifg_p_kernel(
             src = raw[name][:].rearrange("p (t c i) -> p c t i", t=PACK, i=4)[:, part]
             if engine == "scalar":
                 nc.scalar.copy(out=dst, in_=src)
+            elif engine == "gpsimd":
+                nc.gpsimd.tensor_scalar(
+                    staged[name].rearrange("p (m t) -> p m t", t=PACK),
+                    raw[name][:].rearrange("p (t m) -> p m t", t=PACK),
+                    1.0, 0.0, ALU.mult, ALU.add,
+                )
             else:
                 nc.vector.tensor_copy(out=dst, in_=src)
 
@@ -123,10 +131,10 @@ def tile_picked_zlstm_cifg_p_kernel(
         xs_picked = sb("xs_picked", [P, PICKS], U8)
         xs = sb("xs", [P, PICKS], U8)
         es = sb("es", [P, PICKS], U8)
-        xw = sb("xw", [P, PICKS], U32)
+        xw = [sb(f"xw{h}", [P, HALF], U32) for h in range(2)]
         ew = sb("ew", [P, PICKS], U32)
-        for plane in (xs_tab, es_tab):
-            nc.vector.memset(plane[:].bitcast(I32), 0)
+        nc.vector.memset(es_tab[:].bitcast(I32), 0)
+        nc.vector.memset(xs_tab[0:STAGE, :].bitcast(I32), 0)
         warm_in = sb("warm_in", [P, 1], F32)
         warm_out = sb("warm_out", [P, 1], F32)
         nc.vector.memset(warm_in[:], 0.0)
@@ -134,7 +142,7 @@ def tile_picked_zlstm_cifg_p_kernel(
 
         load_weight("vca", vca)
         nc.sync.dma_start(offs_sb[:], offs)
-        nc.scalar.dma_start(out=xs_tab[0:P:8, :].bitcast(I32), in_=x_scales[0].bitcast(I32))
+        nc.scalar.dma_start(out=xs_tab[STAGE:P, :].bitcast(I32), in_=x_scales[0].bitcast(I32))
         nc.sync.dma_start(tok_sb[:], tok)
         nc.scalar.activation(warm_out[:], warm_in[:], ACT.Sigmoid)
         load_words(ew_tab, e_words)
@@ -155,7 +163,7 @@ def tile_picked_zlstm_cifg_p_kernel(
         stage("x", ["wca", "wfo"])
 
         def state_pass(gate, name, h, first):
-            product(gate, name, h, xw[:, cols(h)], xs[:, cols(h)], first)
+            product(gate, name, h, xw[h][:], xs[:, cols(h)], first)
 
         def token_pass(gate, name, h, first):
             product(gate, name, h, ew[:, cols(h)], es[4:P, cols(h)], first)
@@ -172,19 +180,18 @@ def tile_picked_zlstm_cifg_p_kernel(
         cast("wfo", "scalar")
         quantise("x", ["wca", "wfo"])
         for h in range(2):
-            nc.vector.tensor_copy(xw[:, cols(h)], xw_tab[:].bitcast(U32).indirect(entries(offs_sb, h)))
+            nc.vector.tensor_copy(xw[h][:], xw_tab[:].bitcast(U32).indirect(entries(offs_sb, h)))
             state_pass("f", "wfo", h, False)
             state_pass("g", "wca", h, False)
         cast("wex", "scalar")
-        cast("vex", "vector", slice(0, UNITS // 8))
-        cast("vex", "scalar", slice(UNITS // 8, UNITS // 4))
+        cast("vex", "gpsimd")
         quantise("b", ["wex", "vex"])
 
         g = [sb(f"g{h}", [P, HALF], F32) for h in range(2)]
         f = [sb(f"f{h}", [P, HALF], F32) for h in range(2)]
         b = sb("b", [P, PICKS], F32)
         th = sb("th", [P, PICKS], F32)
-        kept = sb("kept", [P, PICKS], F32)
+        kept = [sb(f"kept{h}", [P, HALF], F32) for h in range(2)]
         fresh = sb("fresh", [P, PICKS], F32)
         old = sb("old", [P, HALF], F32)
 
@@ -203,14 +210,16 @@ def tile_picked_zlstm_cifg_p_kernel(
 
         def make_kept(i):
             part = slice(pieces[i].start - HALF, pieces[i].stop - HALF)
-            nc.vector.tensor_tensor(kept[:, pieces[i]], old[:, part], f[1][:, part], ALU.mult)
+            nc.vector.tensor_tensor(kept[1][:, part], old[:, part], f[1][:, part], ALU.mult)
 
         def make_new(i):
             c = pieces[i]
-            nc.vector.tensor_tensor(new[i][:], kept[:, c], fresh[:, c], ALU.subtract)
+            h = c.start // HALF
+            part = slice(c.start - h * HALF, c.stop - h * HALF)
+            nc.vector.tensor_tensor(new[i][:], kept[h][:, part], fresh[:, c], ALU.subtract)
             nc.scalar.activation(th[:, c], new[i][:], ACT.Tanh)
 
-        nc.vector.tensor_tensor(kept[:, cols(0)], cell_sb[:].indirect(entries(offs_sb, 0)), f[0][:], ALU.mult)
+        nc.vector.tensor_tensor(kept[0][:], cell_sb[:].indirect(entries(offs_sb, 0)), f[0][:], ALU.mult)
         for h in range(2):
             state_pass("b", "wex", h, True)
             token_pass("b", "vex", h, False)

@@ -33,7 +33,7 @@ def tile_picked_zlstm_cifg_p_kernel(
         places = {
             "raw_wex": 1984, "xs_tab": 2048, "raw_vex": 6144, "ew_tab": 8128, "cell_sb": 12160, "b": 14208,
             "f0": 1024, "f1": 2048, "g0": 3072, "kept1": 3072, "grouped_b": 24576, "g1": 24576,
-            "codes_x": 16384, "old": 16384, "xw0": 20480, "fresh": 20480,
+            "codes_x": 16384, "old": 16384, "xw0": 20480, "fresh1": 20480, "fresh0": 25600,
         }
 
         def sb(name, shape, dtype):
@@ -192,7 +192,7 @@ def tile_picked_zlstm_cifg_p_kernel(
         b = sb("b", [P, PICKS], F32)
         th = sb("th", [P, PICKS], F32)
         kept = [sb(f"kept{h}", [P, HALF], F32) for h in range(2)]
-        fresh = sb("fresh", [P, PICKS], F32)
+        fresh = [sb(f"fresh{h}", [P, HALF], F32) for h in range(2)]
         old = sb("old", [P, HALF], F32)
 
         nc.scalar.activation(f[0][:], acc["f", 0][:], ACT.Sigmoid)
@@ -206,7 +206,7 @@ def tile_picked_zlstm_cifg_p_kernel(
         res = [sb(f"res{i}", [P, c.stop - c.start], F32) for i, c in enumerate(pieces)]
 
         def make_fresh(h):
-            nc.vector.scalar_tensor_tensor(fresh[:, cols(h)], f[h][:], 1.0, g[h][:], ALU.subtract, ALU.mult)
+            nc.vector.scalar_tensor_tensor(fresh[h][:], f[h][:], 1.0, g[h][:], ALU.subtract, ALU.mult)
 
         def make_kept(i):
             part = slice(pieces[i].start - HALF, pieces[i].stop - HALF)
@@ -216,15 +216,15 @@ def tile_picked_zlstm_cifg_p_kernel(
             c = pieces[i]
             h = c.start // HALF
             part = slice(c.start - h * HALF, c.stop - h * HALF)
-            nc.vector.tensor_tensor(new[i][:], kept[h][:, part], fresh[:, c], ALU.subtract)
+            nc.vector.tensor_tensor(new[i][:], kept[h][:, part], fresh[h][:, part], ALU.subtract)
             nc.scalar.activation(th[:, c], new[i][:], ACT.Tanh)
 
+        make_fresh(0)
         nc.vector.tensor_tensor(kept[0][:], cell_sb[:].indirect(entries(offs_sb, 0)), f[0][:], ALU.mult)
         for h in range(2):
             state_pass("b", "wex", h, True)
             token_pass("b", "vex", h, False)
             nc.scalar.activation(b[:, cols(h)], acc["b", h][:], ACT.Sigmoid)
-        make_fresh(0)
         make_fresh(1)
         make_new(0)
         make_kept(1)

@@ -31,9 +31,9 @@ def tile_picked_zlstm_cifg_p_kernel(
         psum = ctx.enter_context(tc.psum_pool(name="psum", bufs=1))
         reuse = ctx.enter_context(tc.tile_pool(name="reuse", bufs=1))
         places = {
-            "raw_wex": 1984, "xs_tab": 2048, "raw_vex": 6144, "ew_tab": 8128, "cell_sb": 12160, "b": 14208,
-            "f0": 1024, "f1": 2048, "g0": 3072, "kept1": 3072, "grouped_b": 24576, "g1": 24576,
-            "codes_x": 16384, "old": 16384, "xw0": 20480, "fresh1": 20480, "fresh0": 25600,
+            "raw_vex": 6144, "ew_tab": 8128, "cell_sb": 12160, "b": 0,
+            "f0": 1024, "f1": 2048, "g0": 3072, "kept1": 3072, "g1": 7168,
+            "codes_x": 16384, "old": 16384, "xw0": 20480, "fresh1": 20480, "fresh0": 6144,
         }
 
         def sb(name, shape, dtype):
@@ -153,8 +153,8 @@ def tile_picked_zlstm_cifg_p_kernel(
         load_words(xw_tab, x_words)
 
         nc.vector.tensor_copy(xs_picked[:], xs_tab[:].indirect(offs_sb[:]))
-        place_scales(xs, xs_picked, 0)
         load_weight("wex", wex)
+        place_scales(xs, xs_picked, 0)
         load_weight("vex", vex)
         nc.sync.dma_start(out=cell_sb[:], in_=cell)
 
@@ -184,7 +184,7 @@ def tile_picked_zlstm_cifg_p_kernel(
             state_pass("f", "wfo", h, False)
             state_pass("g", "wca", h, False)
         cast("wex", "scalar")
-        cast("vex", "gpsimd")
+        cast("vex", "vector")
         quantise("b", ["wex", "vex"])
 
         g = [sb(f"g{h}", [P, HALF], F32) for h in range(2)]
@@ -222,8 +222,8 @@ def tile_picked_zlstm_cifg_p_kernel(
         make_fresh(0)
         nc.vector.tensor_tensor(kept[0][:], cell_sb[:].indirect(entries(offs_sb, 0)), f[0][:], ALU.mult)
         for h in range(2):
-            state_pass("b", "wex", h, True)
-            token_pass("b", "vex", h, False)
+            token_pass("b", "vex", h, True)
+            state_pass("b", "wex", h, False)
             nc.scalar.activation(b[:, cols(h)], acc["b", h][:], ACT.Sigmoid)
         make_fresh(1)
         make_new(0)

@@ -140,14 +140,14 @@ def tile_picked_zlstm_cifg_p_kernel(
         nc.vector.memset(warm_in[:], 0.0)
         nc.vector.memset(xs[:].bitcast(I32), 0)
 
-        load_weight("vca", vca)
         nc.sync.dma_start(offs_sb[:], offs)
         nc.scalar.dma_start(out=xs_tab[STAGE:P, :].bitcast(I32), in_=x_scales[0].bitcast(I32))
         nc.sync.dma_start(tok_sb[:], tok)
         nc.scalar.activation(warm_out[:], warm_in[:], ACT.Sigmoid)
         load_words(ew_tab, e_words)
-        load_weight("vfo", vfo)
+        load_weight("vca", vca)
         load_scales(es_tab, e_scales, 4)
+        load_weight("vfo", vfo)
         load_weight("wca", wca)
         load_weight("wfo", wfo)
         load_words(xw_tab, x_words)

from contextlib import ExitStack

import concourse.mybir as mybir

F32 = mybir.dt.float32
BF16 = mybir.dt.bfloat16
I32 = mybir.dt.int32
U32 = mybir.dt.uint32
U16 = mybir.dt.uint16
U8 = mybir.dt.uint8
FP8X4 = mybir.dt.float8_e4m3fn_x4
ACT = mybir.ActivationFunctionType
ALU = mybir.AluOpType

P = 128
PACK = 4
TABLE = 1024
PICKS = 512
UNITS = 128
HALF = 256
STAGE = 112
FLOPS = 2 * 6 * 512 * UNITS * PICKS


def tile_picked_zlstm_cifg_p_kernel(
    tc, x_words, x_scales, e_words, e_scales, wfo, vfo, wex, vex, wca, vca, cell, offs, tok, out
):
    nc = tc.nc
    with ExitStack() as ctx:
        keep = ctx.enter_context(tc.tile_pool(name="keep", bufs=1))
        psum = ctx.enter_context(tc.psum_pool(name="psum", bufs=1))
        reuse = ctx.enter_context(tc.tile_pool(name="reuse", bufs=1))
        places = {
            "raw_vex": 6144, "ew_tab": 8128, "cell_sb": 12160, "b": 0,
            "f0": 1024, "f1": 2048, "g0": 3072, "kept1": 3072, "g1": 7168,
            "codes_x": 16384, "old": 16384, "xw0": 20480, "fresh1": 20480, "fresh0": 6144,
        }

        def sb(name, shape, dtype):
            if name in places:
                return reuse.tile(shape, dtype, name=name, align_bytes=64, offset=places[name])
            return keep.tile(shape, dtype, name=name, align_bytes=64)

        offs_sb = keep.tile([P, PICKS // 16], U16, name="offs_sb")
        tok_sb = keep.tile([P, PICKS // 16], U16, name="tok_sb")
        xs_tab = sb("xs_tab", [P, TABLE], U8)
        es_tab = sb("es_tab", [P, TABLE], U8)
        xw_tab = sb("xw_tab", [P, TABLE], I32)
        ew_tab = sb("ew_tab", [P, TABLE], I32)
        cell_sb = sb("cell_sb", [P, TABLE], F32)

        def load_scales(table, scales, first):
            for r in range(4):
                nc.sync.dma_start(
                    out=table[first + r : P : 32, :].bitcast(I32),
                    in_=scales[0, r : 16 : 4, :].bitcast(I32),
                )

        def place_scales(plane, picked, first):
            for r in range(4):
                nc.sync.dma_start(
                    out=plane[first + r : P : 32, :].bitcast(I32),
                    in_=picked[STAGE + r : P : 4, :].bitcast(I32),
                )

        def load_words(table, words):
            nc.sync.dma_start(out=table[:], in_=words[0].rearrange("p n t -> p (n t)").bitcast(I32))

        raw = {}

        def load_weight(name, w):
            raw[name] = sb("raw_" + name, [P, PACK * UNITS], F32)
            nc.sync.dma_start(out=raw[name][:], in_=w.rearrange("(p j) m -> p (j m)", j=PACK))

        codes, scales, staged = {}, {}, {}

        def stage(group, names):
            tile = sb("grouped_" + group, [P, len(names) * UNITS * PACK], BF16)
            for i, name in enumerate(names):
                staged[name] = tile[:, i * UNITS * PACK : (i + 1) * UNITS * PACK]
            staged[group] = tile[:]

        def cast(name, engine, part=slice(0, UNITS // 4)):
            dst = staged[name].rearrange("p (c i t) -> p c t i", i=4, t=PACK)[:, part]
            src = raw[name][:].rearrange("p (t c i) -> p c t i", t=PACK, i=4)[:, part]
            if engine == "scalar":
                nc.scalar.copy(out=dst, in_=src)
            elif engine == "gpsimd":
                nc.gpsimd.tensor_scalar(
                    staged[name].rearrange("p (m t) -> p m t", t=PACK),
                    raw[name][:].rearrange("p (t m) -> p m t", t=PACK),
                    1.0, 0.0, ALU.mult, ALU.add,
                )
            else:
                nc.vector.tensor_copy(out=dst, in_=src)

        def quantise(group, names):
            n = len(names)
            cw = sb("codes_" + group, [P, n * UNITS], U32)
            cs = sb("scales_" + group, [P, n * UNITS], U8)
            nc.vector.quantize_mx(out=cw[:].bitcast(FP8X4), scales=cs[:], in_=staged[group])
            for i, name in enumerate(names):
                codes[name] = cw[:, i * UNITS : (i + 1) * UNITS]
                scales[name] = cs[:, i * UNITS : (i + 1) * UNITS]

        acc = {}

        def product(gate, name, h, words, bytes_, first):
            if first:
                acc[gate, h] = psum.tile([P, HALF], F32, name=f"acc_{gate}{h}")
            nc.tensor.matmul_mx(
                out=acc[gate, h][:],
                lhsT=codes[name].bitcast(FP8X4),
                lhsT_scale=scales[name],
                rhs=words.bitcast(FP8X4),
                rhs_scale=bytes_,
                start=first,
                stop=not first,
            )

        def cols(h):
            return slice(h * HALF, (h + 1) * HALF)

        def entries(lst, h):
            return lst[:, h * HALF // 16 : (h + 1) * HALF // 16]

        def clock(name, ap):
            c = sb("clock_" + name, [P, 1], ap.dtype)
            nc.gpsimd.tensor_copy(c[:], ap)

        xs_picked = sb("xs_picked", [P, PICKS], U8)
        xs = sb("xs", [P, PICKS], U8)
        es = sb("es", [P, PICKS], U8)
        xw = [sb(f"xw{h}", [P, HALF], U32) for h in range(2)]
        ew = sb("ew", [P, PICKS], U32)
        nc.vector.memset(es_tab[:].bitcast(I32), 0)
        nc.vector.memset(xs_tab[0:STAGE, :].bitcast(I32), 0)
        warm_in = sb("warm_in", [P, 1], F32)
        warm_out = sb("warm_out", [P, 1], F32)
        nc.vector.memset(warm_in[:], 0.0)
        nc.vector.memset(xs[:].bitcast(I32), 0)

        nc.sync.dma_start(offs_sb[:], offs)
        nc.scalar.dma_start(out=xs_tab[STAGE:P, :].bitcast(I32), in_=x_scales[0].bitcast(I32))
        nc.sync.dma_start(tok_sb[:], tok)
        nc.scalar.activation(warm_out[:], warm_in[:], ACT.Sigmoid)
        load_words(ew_tab, e_words)
        load_weight("vca", vca)
        load_scales(es_tab, e_scales, 4)
        load_weight("vfo", vfo)
        load_weight("wca", wca)
        load_weight("wfo", wfo)
        load_words(xw_tab, x_words)

        nc.vector.tensor_copy(xs_picked[:], xs_tab[:].indirect(offs_sb[:]))
        load_weight("wex", wex)
        place_scales(xs, xs_picked, 0)
        load_weight("vex", vex)
        nc.sync.dma_start(out=cell_sb[:], in_=cell)

        stage("e", ["vca", "vfo"])
        stage("b", ["wex", "vex"])
        stage("x", ["wca", "wfo"])

        def state_pass(gate, name, h, first):
            product(gate, name, h, xw[h][:], xs[:, cols(h)], first)

        def token_pass(gate, name, h, first):
            product(gate, name, h, ew[:, cols(h)], es[4:P, cols(h)], first)

        cast("vca", "scalar")
        cast("vfo", "scalar")
        nc.vector.tensor_copy(ew[:], ew_tab[:].bitcast(U32).indirect(tok_sb[:]))
        quantise("e", ["vca", "vfo"])
        for h in range(2):
            nc.vector.tensor_copy(es[:, cols(h)], es_tab[:].indirect(entries(tok_sb, h)))
            token_pass("f", "vfo", h, True)
            token_pass("g", "vca", h, True)
        cast("wca", "scalar")
        cast("wfo", "scalar")
        quantise("x", ["wca", "wfo"])
        for h in range(2):
            nc.vector.tensor_copy(xw[h][:], xw_tab[:].bitcast(U32).indirect(entries(offs_sb, h)))
            state_pass("f", "wfo", h, False)
            state_pass("g", "wca", h, False)
        cast("wex", "scalar")
        cast("vex", "vector")
        quantise("b", ["wex", "vex"])

        g = [sb(f"g{h}", [P, HALF], F32) for h in range(2)]
        f = [sb(f"f{h}", [P, HALF], F32) for h in range(2)]
        b = sb("b", [P, PICKS], F32)
        th = sb("th", [P, PICKS], F32)
        kept = [sb(f"kept{h}", [P, HALF], F32) for h in range(2)]
        fresh = [sb(f"fresh{h}", [P, HALF], F32) for h in range(2)]
        old = sb("old", [P, HALF], F32)

        nc.scalar.activation(f[0][:], acc["f", 0][:], ACT.Sigmoid)
        nc.scalar.activation(g[0][:], acc["g", 0][:], ACT.Tanh)
        nc.scalar.activation(f[1][:], acc["f", 1][:], ACT.Sigmoid)
        nc.scalar.activation(g[1][:], acc["g", 1][:], ACT.Tanh)
        nc.scalar.activation(old[:], cell_sb[:].indirect(entries(offs_sb, 1)), ACT.Copy)

        pieces = [slice(0, HALF), slice(HALF, HALF + UNITS), slice(HALF + UNITS, PICKS)]
        new = [sb(f"new{i}", [P, c.stop - c.start], F32) for i, c in enumerate(pieces)]
        res = [sb(f"res{i}", [P, c.stop - c.start], F32) for i, c in enumerate(pieces)]

        def make_fresh(h):
            nc.vector.scalar_tensor_tensor(fresh[h][:], f[h][:], 1.0, g[h][:], ALU.subtract, ALU.mult)

        def make_kept(i):
            part = slice(pieces[i].start - HALF, pieces[i].stop - HALF)
            nc.vector.tensor_tensor(kept[1][:, part], old[:, part], f[1][:, part], ALU.mult)

        def make_new(i):
            c = pieces[i]
            h = c.start // HALF
            part = slice(c.start - h * HALF, c.stop - h * HALF)
            nc.vector.tensor_tensor(new[i][:], kept[h][:, part], fresh[h][:, part], ALU.subtract)
            nc.scalar.activation(th[:, c], new[i][:], ACT.Tanh)

        make_fresh(0)
        nc.vector.tensor_tensor(kept[0][:], cell_sb[:].indirect(entries(offs_sb, 0)), f[0][:], ALU.mult)
        for h in range(2):
            token_pass("b", "vex", h, True)
            state_pass("b", "wex", h, False)
            nc.scalar.activation(b[:, cols(h)], acc["b", h][:], ACT.Sigmoid)
        make_fresh(1)
        make_new(0)
        make_kept(1)
        make_kept(2)
        make_new(1)
        make_new(2)
        for i, c in enumerate(pieces):
            nc.vector.tensor_tensor(res[i][:], b[:, c], th[:, c], ALU.mult)
            nc.sync.dma_start(out=out[:, c], in_=res[i][:])
